import numpy as np, ml_dtypes
CORES = [12,28,60,100,156,228]
N = 6
import mx_ref
BF = ml_dtypes.bfloat16
def entries(a):
    return np.ascontiguousarray(a.T).reshape(-1)
def table(e):
    return np.ascontiguousarray(np.reshape(e, (-1, 16)).T).astype(np.int32)
def cols(t, e):
    v = np.concatenate([t.reshape(128, -1, 4), np.zeros((128, 1, 4), BF)], axis=1)
    return np.ascontiguousarray(v[:, e]).reshape(128, -1)
def f(rng, *shape):
    return mx_ref.flush((rng.standard_normal(shape, dtype=np.float32) * np.exp2(rng.integers(-2, 3, shape[:-1] + (1,)))).astype(BF))
def wide(rng, *shape, cols=0):
    v = rng.standard_normal(shape, dtype=np.float32) * np.exp2(rng.integers(-12, 13, shape)).astype(np.float32)
    if cols: v *= np.repeat(np.exp2(rng.integers(-cols, cols + 1, shape[:-2] + (1, shape[-1] // 4))) * (rng.random(shape[:-2] + (1, shape[-1] // 4)) > 0.0625), 4, axis=-1).astype(np.float32)
    return mx_ref.flush(v.astype(BF))
T, S, CAPP = 512, 192, 48
def lists(rng, most=None, own=False, share=False, edge=False):
    o, c, m = [], [], []
    for r in range(N):
        n = np.zeros(N, int)
        if own: n[r] = CAPP
        if most is not None:
            for q in rng.permutation(N)[:most]: n[q] = CAPP
            n = np.minimum(n, np.maximum(0, S - (np.cumsum(n) - n)))
        while n.sum() < S:
            q = rng.integers(0, N)
            if n[q] < CAPP: n[q] += 1
        slots = np.full(N * CAPP, -1); used = []
        for q in range(N):
            k = q * CAPP + rng.permutation(CAPP)[:n[q]]; used += list(k)
            slots[k] = rng.integers(0, T) if share else rng.choice([0, T - 1], n[q]) if edge else rng.integers(0, T, n[q])
        o.append(table(rng.choice([0, T - 1], S) if edge else rng.integers(0, T, S))); c.append(table(slots)); m.append(table(rng.permutation(used)))
    return {"own": np.stack(o), "want": np.stack(c), "slot": np.stack(m)}
def setup_inputs(rng):
    return {"x": f(rng, N, 128, 4 * T), "w": f(rng, N, 128, 512), **lists(rng)}
def setup_inputs_edge(rng):
    return {**setup_inputs(rng), **lists(rng, edge=True)}
def setup_inputs_full(rng):
    return {**setup_inputs(rng), **lists(rng, most=S // CAPP)}
def setup_inputs_self(rng):
    return {**setup_inputs(rng), **lists(rng, own=True)}
def setup_inputs_share(rng):
    return {**setup_inputs(rng), **lists(rng, share=True)}
def setup_inputs_spread(rng):
    d = setup_inputs(rng); d["x"] = wide(rng, N, 128, 4 * T, cols=8); return d
def check_inputs(d):
    b = []
    for r in range(N):
        o, c, m = entries(d["own"][r]), entries(d["want"][r]), entries(d["slot"][r])
        if o.min() < 0 or o.max() >= T: b.append("own")
        if c.min() < -1 or c.max() >= T: b.append("want")
        if m.min() < 0 or m.max() >= N * CAPP or len(set(m.tolist())) != S or (c[m] < 0).any() or (c >= 0).sum() != S: b.append("slot")
    return b
def decode(q):
    out = np.zeros(q[0].shape, np.float32)
    for b in range(4):
        e = np.zeros((128, 128, 4), np.float32); e[np.arange(128), np.arange(128), b] = 1
        out[:, b::4] = mx_ref.matmul(mx_ref.quantize(e.reshape(128, 512).astype(BF)), q)
    return out
def reference(x, w, own, want, slot):
    M = []
    for r in range(N):
        c = entries(want[r])
        arrived = np.concatenate([decode(mx_ref.quantize(cols(x[q], c[q * CAPP:(q + 1) * CAPP]))) for q in range(N)], axis=1)
        far = arrived.reshape(128, -1, 4)[:, entries(slot[r])].reshape(128, -1)
        M.append(mx_ref.quantize(((cols(x[r], entries(own[r])).astype(np.float32) + far) * np.float32(0.5)).astype(BF)))
    y = np.zeros((N, 128, 3 * S), np.float32)
    for r in range(N):
        for i in range(3): y[r][:, S * i:S * i + S] = mx_ref.matmul(mx_ref.quantize(w[r]), M[(r - 1 + i) % N])
    return {"y": y}

@@ -1,0 +1,361 @@
+from concourse.bass import DstId, RemoteDMATransfer
+from concourse.mybir import dt, AluOpType, ActivationFunctionType
+
+N, T_COLS, S, CAP = 6, 512, 192, 48
+K = CAP // 16
+W4 = 4 * T_COLS
+F_W = N * CAP
+
+X4, U8 = "float8_e4m3fn_x4", "uint8"
+SCRATCH = {
+    "xs": ("sbuf", [128, W4], "bfloat16"),
+    "wt": ("sbuf", [128, 512], "bfloat16"),
+    "wl": ("sbuf", [128, K * N], "int32"),
+    "ol": ("sbuf", [128, S // 16], "int32"),
+    "sl": ("sbuf", [128, S // 16], "int32"),
+    "wu": ("sbuf", [128, K * N], "uint16"),
+    "su": ("sbuf", [128, 4], "uint16"),
+    "ou": ("sbuf", [128, S // 16], "uint16"),
+    "so": ("sbuf", [128, S // 16], "uint16"),
+    "ta": ("sbuf", [128, S // 16], "int32"),
+    "tb": ("sbuf", [128, S // 16], "int32"),
+    "tc": ("sbuf", [128, S // 16], "int32"),
+    "td": ("sbuf", [128, S // 16], "int32"),
+    "te": ("sbuf", [128, S // 16], "int32"),
+    "tf": ("sbuf", [128, S // 16], "int32"),
+    "li": ("sbuf", [128, 12], "uint16"),
+    "lj": ("sbuf", [128, 12], "uint16"),
+    "half": ("sbuf", [128, 128], "bfloat16"),
+    "idt": ("sbuf", [128, 128], "bfloat16"),
+    "e4": ("sbuf", [128, 2048], "bfloat16"),
+    "qe": ("sbuf", [128, 512], X4),
+    "qes": ("sbuf", [128, 512], U8),
+    "wq": ("sbuf", [128, 128], X4),
+    "wqs": ("sbuf", [128, 128], U8),
+    "ga": ("sbuf", [128, 4 * 144], "bfloat16"),
+    "gx": ("sbuf", [128, 4 * 192], "bfloat16"),
+    "ac": ("sbuf", [128, 384], X4),
+    "acs": ("sbuf", [128, 384], U8),
+    "qx": ("sbuf", [128, 192], X4),
+    "qxs": ("sbuf", [128, 192], U8),
+    "oh": ("sbuf", [128, 4 * S], "bfloat16"),
+    "ft": ("sbuf", [128, 4 * F_W], "bfloat16"),
+    "mt": ("sbuf", [128, 4 * S], "bfloat16"),
+    "qm": ("sbuf", [128, S], X4),
+    "qms": ("sbuf", [128, S], U8),
+    "ml": ("sbuf", [128, S], X4),
+    "mls": ("sbuf", [128, S], U8),
+    "mr": ("sbuf", [128, S], X4),
+    "mrs": ("sbuf", [128, S], U8),
+    "yb": ("sbuf", [128, 3 * S], "float32"),
+    "rl": ("sbuf", [128, K * N], "uint16"),
+    "rc": ("sbuf", [128, 2 * CAP], X4),
+    "rcs": ("sbuf", [128, 2 * CAP], U8),
+    "rm": ("sbuf", [128, S], X4),
+    "rms": ("sbuf", [128, S], U8),
+    "pe": ("psum", [128, 2048], "float32"),
+    "pl": ("psum", [128, 2048], "float32"),
+}
+CODES = {k for k, v in SCRATCH.items() if v[2] == X4}
+ARRIVALS = ["a_li", "a_lj", "a_ce", "a_cl", "a_ml", "a_mr", "r_l", "r_c", "r_cs", "r_m", "r_ms"]
+EVENTS = (["ldw", "ldx", "ldo", "lds", "ldwt", "half", "e0", "pad", "idt", "wu", "su", "ou", "e1", "qe", "gs", "ge", "qearly",
+           "gl", "qlate", "oh", "s1", "s2", "s3", "s4", "s5", "wq", "fe", "ma", "mq", "yst", "sent"]
+          + ["me%d" % b for b in range(4)] + ["mlt%d" % b for b in range(4)] + ["fl%d" % b for b in range(4)]
+          + ["y%d" % i for i in range(3)] + ["yc%d" % i for i in range(3)])
+SEMAPHORES = ARRIVALS + EVENTS
+
+
+def deal(engines, k, back=False):
+    n = len(engines)
+    sizes = [n // 2, n // 4, n // 4] if k == 3 else [n // k] * k
+    if back:
+        sizes = sizes[::-1]
+    out, a = [], 0
+    for s in sizes:
+        out.append(engines[a:a + s])
+        a += s
+    return out
+
+
+def groups(cores, topo):
+    direct = [[q for q in range(N) if q != r and topo.may_write(cores[r], cores[q])] for r in range(N)]
+    cross = [[q for q in range(N) if q != r and q not in direct[r]] for r in range(N)]
+    return direct, cross
+
+
+def layout(r, direct, cross):
+    A, X = ("ga", "ac", "acs"), ("gx", "qx", "qxs")
+    ne, nl = CAP * len(direct[r]), CAP * len(cross[r])
+    if ne >= 128:
+        na, nx, pad = nl + CAP, ne, 0
+        early, late, me = X + (0,), A + (0,), nl
+    else:
+        na, nx = 128, nl
+        pad = na - CAP - ne
+        early, late, me = A + (pad,), X + (0,), pad + ne
+    return {"na": na, "nx": nx, "pad": pad, "early": early, "late": late, "self": me, "ein": na, "lin": na + ne,
+            "ne": ne, "nl": nl, "early_is_x": ne >= 128}
+
+
+def make_plan(cores, topo):
+    direct, cross = groups(cores, topo)
+    lay = [layout(r, direct, cross) for r in range(N)]
+    calls, due = {}, {}
+
+    def call(core, tag, trs):
+        calls.setdefault(core, []).append((tag, trs))
+        for to, eng, src, dst, sem in trs:
+            due[(to, sem)] = due.get((to, sem), 0) + len(eng)
+
+    for r in range(N):
+        c, L = cores[r], lay[r]
+        D, X = direct[r], cross[r]
+        ports = [p for p in topo.cores_of(c) if p != c and topo.may_write(p, cores[X[0]])]
+        near = [p for p in ports if topo.die(p) == topo.die(c)]
+        far = [p for p in ports if topo.die(p) != topo.die(c)]
+        rel = [near[0], far[0], far[1], near[1]][:len(X)]
+        out = topo.engines(c, cores[D[0]])
+        every = topo.engines(c, rel[0])
+        inside = [e for e in every if e not in out]
+        four = len(rel) == 4
+
+        def away(p):
+            return topo.engines(p, cores[X[0]])
+
+        sh = deal(inside, len(rel))
+        call(c, "list", [(p, sh[i], ("wu", 0, K * N), ("rl", 0, K * N), "r_l") for i, p in enumerate(rel)])
+        for i, p in enumerate(rel):
+            q = X[i]
+            j = cross[q].index(r)
+            call(p, "r_l", [(cores[q], away(p), ("rl", K * q, K * q + K), ("lj", K * j, K * j + K), "a_lj")])
+        sh = deal(out, len(D))
+        call(c, "list", [(cores[q], sh[i], ("wu", K * q, K * q + K),
+                          ("li", K * direct[q].index(r), K * direct[q].index(r) + K), "a_li") for i, q in enumerate(D)])
+
+        def place(buf, q, late):
+            a = lay[q]["lin"] + CAP * cross[q].index(r) if late else lay[q]["ein"] + CAP * direct[q].index(r)
+            return (buf, a, a + CAP)
+
+        for buf, land, back in ((L["early"][1], "ac", False), (L["early"][2], "acs", True)):
+            sh = deal(out, len(D), back)
+            a = L["early"][3]
+            call(c, "early", [(cores[q], sh[i], (buf, a + CAP * i, a + CAP * i + CAP), place(land, q, False), "a_ce")
+                              for i, q in enumerate(D)])
+        a = L["late"][3]
+        if four:
+            parts = [(X[:2], 0, rel[0], rel[2]), (X[2:], 2 * CAP, rel[1], rel[3])]
+        else:
+            flip = (sorted(D + [r]).index(r)) % 2
+            parts = [(X, 0, rel[flip], rel[1 - flip])]
+        ec, es = deal(inside, len(parts)), deal(out if four else inside, len(parts))
+        call(c, "late", [(p[2], ec[i], (L["late"][1], a + p[1], a + p[1] + 2 * CAP), ("rc", 0, 2 * CAP), "r_c")
+                         for i, p in enumerate(parts)])
+        call(c, "late", [(p[3], es[i], (L["late"][2], a + p[1], a + p[1] + 2 * CAP), ("rcs", 0, 2 * CAP), "r_cs")
+                         for i, p in enumerate(parts)])
+        for qs, _, pc, ps in parts:
+            for p, tag, src, land in ((pc, "r_c", "rc", "ac"), (ps, "r_cs", "rcs", "acs")):
+                sh = deal(away(p), len(qs))
+                call(p, tag, [(cores[q], sh[i], (src, CAP * i, CAP * i + CAP), place(land, q, True), "a_cl")
+                              for i, q in enumerate(qs)])
+
+        ways = [((r + 1) % N, "ml", "mls", "a_ml", 0), ((r - 1) % N, "mr", "mrs", "a_mr", 1)]
+        over = [w for w in ways if w[0] in X]
+        here = [w for w in ways if w[0] in D]
+        if over:
+            sh = deal(every, len(over))
+            for b in ((0, 1) if four else (1, 0)):
+                s, l, sem = (("qm", "rm", "r_m"), ("qms", "rms", "r_ms"))[b]
+                via = [rel[w[4] + (2 * b if four else 0)] for w in over]
+                call(c, "m", [(p, sh[i], (s, 0, S), (l, 0, S), sem) for i, p in enumerate(via)])
+                for p, w in zip(via, over):
+                    call(p, sem, [(cores[w[0]], away(p), (l, 0, S), (w[1 + b], 0, S), w[3])])
+        if here:
+            sh = deal(out, len(here))
+            for b in (0, 1):
+                call(c, "m", [(cores[w[0]], sh[i], (("qm", "qms")[b], 0, S), (w[1 + b], 0, S), w[3])
+                              for i, w in enumerate(here)])
+    return direct, cross, lay, calls, due
+
+
+def rank_program(g, core, T, topo):
+    direct, cross, lay, calls, due = make_plan(T.cores, topo)
+    mine = calls.get(core)
+    if mine is None:
+        return
+    count, waited = {}, set()
+
+    def view(v):
+        a = T[v[0]][:, v[1]:v[2]]
+        return a.bitcast(dt.uint8) if v[0] in CODES else a
+
+    def inc(ins, name, n=1):
+        ins.then_inc(T.sem[name], n)
+        count[name] = count.get(name, 0) + n
+
+    def wait(q, *names):
+        for name in names:
+            q.wait_ge(T.sem[name], due[(core, name)] if (core, name) in due else count[name])
+            waited.add(name)
+
+    def send(trs):
+        out = []
+        for to, eng, src, dst, sem in trs:
+            rid, pid = topo.addr(to, core)
+            out.append(RemoteDMATransfer(dst_ids=[DstId(rid=rid, pnc=pid)], dma_engine_mask=sum(1 << e for e in eng),
+                                         remote_sem=T.sem[sem], src=view(src), dst=view(dst)))
+            count["sent"] = count.get("sent", 0) + len(eng)
+        g.remote_dma_fused(out, local_sem=T.sem["sent"])
+
+    def send_all(tag):
+        for t, trs in mine:
+            if t == tag:
+                send(trs)
+
+    r = T.rank_of(core)
+    if r is None:
+        for tag, trs in mine:
+            wait(g, tag)
+            send(trs)
+        wait(g, "sent")
+        return
+
+    vec, act, ten, syn = g.vector, g.scalar, g.tensor, g.sync
+    L, D, X = lay[r], direct[r], cross[r]
+    copy = ActivationFunctionType.Copy
+    add, mult = AluOpType.add, AluOpType.mult
+
+    for k in range(8):
+        inc((syn if k < 4 else act).dma_start(T["wl"][16 * k:16 * k + 16, :], T.want[:]), "ldw", 16)
+    inc(syn.dma_start(T["xs"][:], T.x[:]), "ldx", 16)
+    for k in range(8):
+        inc(act.dma_start(T["ol"][16 * k:16 * k + 16, :], T.own[:]), "ldo", 16)
+    for k in range(8):
+        inc(syn.dma_start(T["sl"][16 * k:16 * k + 16, :], T.slot[:]), "lds", 16)
+    inc(syn.dma_start(T["wt"][:], T.w[:]), "ldwt", 16)
+
+    inc(vec.memset(T["half"][:], 0.5), "half")
+    if L["pad"]:
+        inc(vec.memset(T["ga"][:, 0:4 * L["pad"]], 0.0), "pad")
+    wait(g, "half")
+    inc(g.affine_select(T["idt"][:], T["half"][:], [[-1, 128]], AluOpType.is_equal, 0.0, 0, 1), "idt")
+    wait(vec, "ldw")
+    inc(vec.tensor_scalar(T["wu"][:], T["wl"][:], 0.0, 4.0, AluOpType.max, mult), "wu")
+    wait(g, "wu")
+    send_all("list")
+    inc(vec.tensor_scalar(T["su"][:, 0:K], T["wl"][:, K * r:K * r + K], 0.0, 4.0, AluOpType.max, mult), "su")
+    inc(vec.memset(T["e4"][:], 0.0), "e0")
+    wait(vec, "e0", "idt")
+    for b in range(4):
+        inc(vec.tensor_copy(T["e4"][:, 512 * b + b:512 * b + 512:4], T["idt"][:]), "e1")
+    wait(vec, "e1")
+    inc(vec.quantize_mx(T["qe"][:], T["qes"][:], T["e4"][:]), "qe")
+    wait(vec, "ldo")
+    inc(vec.tensor_scalar(T["ou"][:], T["ol"][:], 4.0, None, mult), "ou")
+
+    def gather(q, tile, a, n, off, t, name):
+        dst = T[tile][:, 4 * a + t:4 * (a + n):4]
+        src = T["xs"][:, t:W4].indirect(T[off][:, 0:n // 16])
+        inc(q.tensor_copy(dst, src) if q is vec else q.activation(dst, src, copy), name)
+
+    wait(act, "su", "ldx")
+    for t in range(4):
+        gather(act, "ga", L["self"], CAP, "su", t, "gs")
+    wait(vec, "ldx")
+    for sem, off, part, n, ev, qev in (("a_li", "li", L["early"], L["ne"], "ge", "qearly"),
+                                       ("a_lj", "lj", L["late"], L["nl"], "gl", "qlate")):
+        wait(vec, sem)
+        wait(act, sem)
+        for t in (0, 1):
+            gather(vec, part[0], part[3], n, off, t, ev)
+            gather(act, part[0], part[3], n, off, t + 2, ev)
+        wait(vec, ev)
+        if part[0] == "ga":
+            wait(vec, "gs")
+            if L["pad"]:
+                wait(vec, "pad")
+        w = L["na"] if part[0] == "ga" else L["nx"]
+        inc(vec.quantize_mx(T[part[1]][:, 0:w], T[part[2]][:, 0:w], T[part[0]][:, 0:4 * w]), qev)
+        wait(g, qev)
+        send_all("early" if ev == "ge" else "late")
+
+    wait(act, "ou")
+    for t in range(4):
+        inc(act.activation(T["oh"][:, S * t:S * t + S], T["xs"][:, t:W4].indirect(T["ou"][:, 0:S // 16]), copy, scale=0.5), "oh")
+    order = sorted(D + [r]) if L["early_is_x"] else X
+    order = order + [q for q in range(N) if q not in order]
+    pos = [order.index(q) for q in range(N)]
+    steps = [(j, pos[j] - pos[j - 1] - 1) for j in range(1, N) if pos[j] - pos[j - 1] != 1]
+    wait(vec, "lds")
+    terms = []
+    for (j, d), tmp in zip(steps, ("ta", "tb", "tc")):
+        inc(vec.tensor_scalar(T[tmp][:], T["sl"][:], float(CAP * j), float(CAP * d), AluOpType.is_ge, mult), "s1")
+        terms.append(tmp)
+    wait(vec, "ldwt")
+    inc(vec.quantize_mx(T["wq"][:], T["wqs"][:], T["wt"][:]), "wq")
+    wait(vec, "s1")
+    acc = "sl"
+    for tmp, to, ev in zip(terms, ("td", "te", "tf"), ("s2", "s3", "s4")):
+        inc(vec.tensor_tensor(T[to][:], T[acc][:], T[tmp][:], add), ev)
+        wait(vec, ev)
+        acc = to
+    inc(vec.tensor_copy(T["so"][:], T[acc][:]), "s5")
+
+    lo, hi = min(L["self"], L["lin"] - 128), L["lin"]
+    wait(ten, "qe", "qlate" if L["early_is_x"] else "qearly", "a_ce")
+    for b in range(4):
+        inc(ten.matmul_mx(T["pe"][:, 512 * b:512 * b + hi - lo], T["qe"][:, 128 * b:128 * b + 128], T["qes"][:, 128 * b:128 * b + 128],
+                          T["ac"][:, lo:hi], T["acs"][:, lo:hi], True, True), "me%d" % b)
+    runs = []
+    for q, a in sorted([(r, L["self"])] + [(q, L["ein"] + CAP * i) for i, q in enumerate(D)], key=lambda v: pos[v[0]]):
+        if runs and runs[-1][0] + runs[-1][2] == a - lo and runs[-1][1] + runs[-1][2] == CAP * pos[q]:
+            runs[-1][2] += CAP
+        else:
+            runs.append([a - lo, CAP * pos[q], CAP])
+
+    def unpack(q, ps, b, a, f, n, ev):
+        dst, src = T["ft"][:, F_W * b + f:F_W * b + f + n], T[ps][:, 512 * b + a:512 * b + a + n]
+        inc(q.tensor_copy(dst, src) if q is vec else q.activation(dst, src, copy), ev)
+
+    for b in range(4):
+        q = vec if b < 2 else act
+        wait(q, "me%d" % b)
+        for a, f, n in runs:
+            unpack(q, "pe", b, a, f, n, "fe")
+
+    end = L["lin"] + L["nl"]
+    lo = min(L["lin"], end - 128)
+    wait(ten, "a_cl")
+    for b in range(4):
+        inc(ten.matmul_mx(T["pl"][:, 512 * b:512 * b + end - lo], T["qe"][:, 128 * b:128 * b + 128], T["qes"][:, 128 * b:128 * b + 128],
+                          T["ac"][:, lo:end], T["acs"][:, lo:end], True, True), "mlt%d" % b)
+    for b in range(4):
+        q = vec if b == 0 else act
+        wait(q, "mlt%d" % b)
+        unpack(q, "pl", b, L["lin"] - lo, CAP * pos[X[0]], L["nl"], "fl%d" % b)
+    wait(vec, "fe", "s5", "oh")
+    for b in range(4):
+        wait(vec, "fl%d" % b)
+        inc(vec.tensor_tensor(T["mt"][:, b:4 * S:4], T["ft"][:, F_W * b:F_W * b + F_W].indirect(T["so"][:, 0:S // 16]),
+                              T["oh"][:, S * b:S * b + S], add), "ma")
+    wait(vec, "ma")
+    inc(vec.quantize_mx(T["qm"][:], T["qms"][:], T["mt"][:]), "mq")
+    wait(g, "mq")
+    send_all("m")
+
+    sides = [(0, "ml", "mls", "a_ml", (r - 1) % N), (2, "mr", "mrs", "a_mr", (r + 1) % N)]
+    sides.sort(key=lambda v: v[4] in X)
+    wait(ten, "wq", "fe", "mq")
+    for i, buf, pl, sem, _ in [(1, "qm", "qms", None, r)] + sides:
+        if sem:
+            wait(ten, sem)
+        inc(ten.matmul_mx(T["pe"][:, 512 * i:512 * i + S], T["wq"][:], T["wqs"][:], T[buf][:], T[pl][:], True, True), "y%d" % i)
+        q, dq = (act, act) if i == 2 else (vec, syn)
+        wait(q, "y%d" % i)
+        dst, src = T["yb"][:, S * i:S * i + S], T["pe"][:, 512 * i:512 * i + S]
+        inc(q.tensor_copy(dst, src) if q is vec else q.activation(dst, src, copy), "yc%d" % i)
+        wait(dq, "yc%d" % i)
+        inc(dq.dma_start(T.y[:, S * i:S * i + S], dst), "yst", 16)
+    wait(g, "yst", "sent")
+    for name in count:
+        if name not in waited:
+            wait(g, name)

@@ -3,31 +3,46 @@ from concourse.mybir import dt, AluOpType, ActivationFunctionType
 
 N, T_COLS, S, CAP = 6, 512, 192, 48
 K = CAP // 16
+KS = S // 16
 W4 = 4 * T_COLS
 F_W = N * CAP
+MIN = 128
+OWN_AT, RIGHT_AT, NB_W = F_W, F_W + S, 2 * F_W + S
 
 X4, U8 = "float8_e4m3fn_x4", "uint8"
 SCRATCH = {
     "xs": ("sbuf", [128, W4], "bfloat16"),
     "wt": ("sbuf", [128, 512], "bfloat16"),
     "wl": ("sbuf", [128, K * N], "int32"),
-    "ol": ("sbuf", [128, S // 16], "int32"),
-    "sl": ("sbuf", [128, S // 16], "int32"),
+    "ls": ("sbuf", [128, 2 * KS], "int32"),
     "wu": ("sbuf", [128, K * N], "uint16"),
     "su": ("sbuf", [128, 4], "uint16"),
-    "ou": ("sbuf", [128, S // 16], "uint16"),
-    "so": ("sbuf", [128, S // 16], "uint16"),
-    "ta": ("sbuf", [128, S // 16], "int32"),
-    "tb": ("sbuf", [128, S // 16], "int32"),
-    "tc": ("sbuf", [128, S // 16], "int32"),
-    "td": ("sbuf", [128, S // 16], "int32"),
-    "te": ("sbuf", [128, S // 16], "int32"),
-    "tf": ("sbuf", [128, S // 16], "int32"),
+    "ou": ("sbuf", [128, KS], "uint16"),
+    "so": ("sbuf", [128, KS], "uint16"),
+    "sm": ("sbuf", [128, KS], "uint16"),
+    "oo": ("sbuf", [128, K * N], "uint16"),
+    "t0": ("sbuf", [128, KS], "int32"),
+    "t1": ("sbuf", [128, KS], "int32"),
+    "t2": ("sbuf", [128, KS], "int32"),
+    "t3": ("sbuf", [128, KS], "int32"),
+    "t4": ("sbuf", [128, KS], "int32"),
+    "t5": ("sbuf", [128, KS], "int32"),
+    "t6": ("sbuf", [128, KS], "int32"),
+    "cnt": ("sbuf", [128, T_COLS], "float32"),
+    "pcol": ("sbuf", [128, 1], "float32"),
+    "m0": ("sbuf", [128, 16], "int32"),
+    "m1": ("sbuf", [128, 16], "int32"),
+    "m16": ("sbuf", [128, 16], "float32"),
+    "keep": ("sbuf", [128, F_W], "bfloat16"),
+    "orow": ("sbuf", [128, S], "float32"),
+    "omask": ("sbuf", [128, S], "float32"),
+    "rrow": ("sbuf", [128, F_W], "float32"),
+    "rsum": ("sbuf", [128, F_W], "float32"),
     "li": ("sbuf", [128, 12], "uint16"),
     "lj": ("sbuf", [128, 12], "uint16"),
-    "half": ("sbuf", [128, 128], "bfloat16"),
-    "idt": ("sbuf", [128, 128], "bfloat16"),
-    "e4": ("sbuf", [128, 2048], "bfloat16"),
+    "sl": ("sbuf", [128, KS], "uint16"),
+    "sr": ("sbuf", [128, KS], "uint16"),
+    "diag": ("sbuf", [128, 516], "bfloat16"),
     "qe": ("sbuf", [128, 512], X4),
     "qes": ("sbuf", [128, 512], U8),
     "wq": ("sbuf", [128, 128], X4),
@@ -38,30 +53,36 @@ SCRATCH = {
     "acs": ("sbuf", [128, 384], U8),
     "qx": ("sbuf", [128, 192], X4),
     "qxs": ("sbuf", [128, 192], U8),
-    "oh": ("sbuf", [128, 4 * S], "bfloat16"),
-    "ft": ("sbuf", [128, 4 * F_W], "bfloat16"),
-    "mt": ("sbuf", [128, 4 * S], "bfloat16"),
-    "qm": ("sbuf", [128, S], X4),
-    "qms": ("sbuf", [128, S], U8),
-    "ml": ("sbuf", [128, S], X4),
-    "mls": ("sbuf", [128, S], U8),
-    "mr": ("sbuf", [128, S], X4),
-    "mrs": ("sbuf", [128, S], U8),
+    "oh": ("sbuf", [128, 4 * F_W], "bfloat16"),
+    "mt": ("sbuf", [128, 4 * (F_W + 32)], "bfloat16"),
+    "nb": ("sbuf", [128, NB_W], X4),
+    "nbs": ("sbuf", [128, NB_W], U8),
+    "ql": ("sbuf", [128, S], X4),
+    "qls": ("sbuf", [128, S], U8),
+    "yt0": ("sbuf", [128, F_W], "float32"),
+    "yt1": ("sbuf", [128, F_W], "float32"),
+    "yt2": ("sbuf", [128, F_W], "float32"),
     "yb": ("sbuf", [128, 3 * S], "float32"),
-    "rl": ("sbuf", [128, K * N], "uint16"),
+    "rl": ("sbuf", [128, K], "uint16"),
+    "rs": ("sbuf", [128, KS], "uint16"),
     "rc": ("sbuf", [128, 2 * CAP], X4),
     "rcs": ("sbuf", [128, 2 * CAP], U8),
+    "rd": ("sbuf", [128, CAP], X4),
+    "rds": ("sbuf", [128, CAP], U8),
+    "re": ("sbuf", [128, S], X4),
+    "res": ("sbuf", [128, S], U8),
     "rm": ("sbuf", [128, S], X4),
     "rms": ("sbuf", [128, S], U8),
     "pe": ("psum", [128, 2048], "float32"),
     "pl": ("psum", [128, 2048], "float32"),
 }
 CODES = {k for k, v in SCRATCH.items() if v[2] == X4}
-ARRIVALS = ["a_li", "a_lj", "a_ce", "a_cl", "a_ml", "a_mr", "r_l", "r_c", "r_cs", "r_m", "r_ms"]
-EVENTS = (["ldw", "ldx", "ldo", "lds", "ldwt", "half", "e0", "pad", "idt", "wu", "su", "ou", "e1", "qe", "gs", "ge", "qearly",
-           "gl", "qlate", "oh", "s1", "s2", "s3", "s4", "s5", "wq", "fe", "ma", "mq", "yst", "sent"]
-          + ["me%d" % b for b in range(4)] + ["mlt%d" % b for b in range(4)] + ["fl%d" % b for b in range(4)]
-          + ["y%d" % i for i in range(3)] + ["yc%d" % i for i in range(3)])
+ARRIVALS = ["a_li", "a_lj", "a_sl", "a_sr", "a_ce", "a_cl", "a_le", "a_re", "a_ll", "a_rl", "r_l", "r_s", "r_d", "r_c", "r_e", "r_m"]
+EVENTS = (["ldw", "ldx", "ldl", "ldwt", "z0", "z1", "z2", "pad", "io0", "io1", "io2", "cnt", "diag", "m1", "m16", "wu", "su",
+           "d1", "d2", "ou", "s1", "s2", "s3", "s4", "s5", "so", "sm", "orow", "omask", "rrow", "rsum", "oo", "qe", "gs", "ge",
+           "qearly", "gl", "qlate", "ohe", "ohl", "wq", "mae", "mal", "mqe", "mql", "yst", "sent"]
+          + ["me%d" % b for b in range(4)] + ["ml%d" % b for b in range(4)]
+          + [s % i for s in ("ye%d", "yl%d", "ce%d", "cl%d", "yg%d") for i in range(3)])
 SEMAPHORES = ARRIVALS + EVENTS
 
 
@@ -77,29 +98,48 @@ def deal(engines, k, back=False):
     return out
 
 
+def orders(items):
+    if len(items) < 2:
+        return [list(items)]
+    return [[v] + rest for i, v in enumerate(items) for rest in orders(items[:i] + items[i + 1:])]
+
+
+def jumps(pos):
+    return [(j, pos[j] - pos[j - 1] - 1) for j in range(1, N) if pos[j] - pos[j - 1] != 1]
+
+
 def groups(cores, topo):
-    direct = [[q for q in range(N) if q != r and topo.may_write(cores[r], cores[q])] for r in range(N)]
-    cross = [[q for q in range(N) if q != r and q not in direct[r]] for r in range(N)]
-    return direct, cross
+    near = [q for q in range(N) if q == 0 or topo.may_write(cores[0], cores[q])]
+    far = [q for q in range(N) if q not in near]
+    wide, narrow = sorted((near, far), key=len, reverse=True)
+    order = min((a + b for a in orders(wide) for b in orders(narrow)), key=lambda o: len(jumps([o.index(q) for q in range(N)])))
+    direct = [[q for q in order if q != r and topo.may_write(cores[r], cores[q])] for r in range(N)]
+    cross = [[q for q in order if q != r and q not in direct[r]] for r in range(N)]
+    return direct, cross, [order.index(q) for q in range(N)]
 
 
-def layout(r, direct, cross):
+def layout(r, direct, cross, pos):
     A, X = ("ga", "ac", "acs"), ("gx", "qx", "qxs")
     ne, nl = CAP * len(direct[r]), CAP * len(cross[r])
-    if ne >= 128:
+    if ne >= MIN:
         na, nx, pad = nl + CAP, ne, 0
         early, late, me = X + (0,), A + (0,), nl
     else:
-        na, nx = 128, nl
+        na, nx = MIN, nl
         pad = na - CAP - ne
         early, late, me = A + (pad,), X + (0,), pad + ne
     return {"na": na, "nx": nx, "pad": pad, "early": early, "late": late, "self": me, "ein": na, "lin": na + ne,
-            "ne": ne, "nl": nl, "early_is_x": ne >= 128}
+            "ne": ne, "nl": nl, "early_is_x": ne >= MIN,
+            "e0": CAP * min(pos[q] for q in direct[r] + [r]), "we": ne + CAP, "l0": CAP * pos[cross[r][0]], "wl": nl}
+
+
+def landing(L, side):
+    return (L["wl"], 0) if side == 0 else (RIGHT_AT, RIGHT_AT + L["we"])
 
 
 def make_plan(cores, topo):
-    direct, cross = groups(cores, topo)
-    lay = [layout(r, direct, cross) for r in range(N)]
+    direct, cross, pos = groups(cores, topo)
+    lay = [layout(r, direct, cross, pos) for r in range(N)]
     calls, due = {}, {}
 
     def call(core, tag, trs):
@@ -113,72 +153,83 @@ def make_plan(cores, topo):
         ports = [p for p in topo.cores_of(c) if p != c and topo.may_write(p, cores[X[0]])]
         near = [p for p in ports if topo.die(p) == topo.die(c)]
         far = [p for p in ports if topo.die(p) != topo.die(c)]
-        rel = [near[0], far[0], far[1], near[1]][:len(X)]
+        rel = [near[0], far[0], far[1], near[1]]
         out = topo.engines(c, cores[D[0]])
         every = topo.engines(c, rel[0])
         inside = [e for e in every if e not in out]
-        four = len(rel) == 4
+        ways = [((r + 1) % N, 0, "l"), ((r - 1) % N, 2, "r")]
 
         def away(p):
             return topo.engines(p, cores[X[0]])
 
-        sh = deal(inside, len(rel))
-        call(c, "list", [(p, sh[i], ("wu", 0, K * N), ("rl", 0, K * N), "r_l") for i, p in enumerate(rel)])
-        for i, p in enumerate(rel):
-            q = X[i]
+        sh = deal(inside, len(X))
+        call(c, "list", [(rel[i], sh[i], ("wu", K * q, K * q + K), ("rl", 0, K), "r_l") for i, q in enumerate(X)])
+        for i, q in enumerate(X):
             j = cross[q].index(r)
-            call(p, "r_l", [(cores[q], away(p), ("rl", K * q, K * q + K), ("lj", K * j, K * j + K), "a_lj")])
-        sh = deal(out, len(D))
-        call(c, "list", [(cores[q], sh[i], ("wu", K * q, K * q + K),
-                          ("li", K * direct[q].index(r), K * direct[q].index(r) + K), "a_li") for i, q in enumerate(D)])
+            call(rel[i], "r_l", [(cores[q], away(rel[i]), ("rl", 0, K), ("lj", K * j, K * j + K), "a_lj")])
+        plane = sorted(D + [r])
+        third = [plane[(plane.index(r) + 2) % len(plane)]] if len(D) > 2 else []
+        pair = [q for q in D if q not in third]
+        for some in (pair, third):
+            if some:
+                sh = deal(out, len(some))
+                call(c, "list", [(cores[q], sh[i], ("wu", K * q, K * q + K),
+                                  ("li", K * direct[q].index(r), K * direct[q].index(r) + K), "a_li") for i, q in enumerate(some)])
+        sh = deal(inside, 2)
+        call(c, "slot", [(rel[3 - i], sh[i], ("so", 0, KS), ("rs", 0, KS), "r_s") for i in range(2)])
+        for i, (q, side, n) in enumerate(ways):
+            call(rel[3 - i], "r_s", [(cores[q], away(rel[3 - i]), ("rs", 0, KS), ("s" + n, 0, KS), "a_s" + n)])
 
         def place(buf, q, late):
             a = lay[q]["lin"] + CAP * cross[q].index(r) if late else lay[q]["ein"] + CAP * direct[q].index(r)
             return (buf, a, a + CAP)
 
-        for buf, land, back in ((L["early"][1], "ac", False), (L["early"][2], "acs", True)):
-            sh = deal(out, len(D), back)
-            a = L["early"][3]
-            call(c, "early", [(cores[q], sh[i], (buf, a + CAP * i, a + CAP * i + CAP), place(land, q, False), "a_ce")
-                              for i, q in enumerate(D)])
-        a = L["late"][3]
-        if four:
-            parts = [(X[:2], 0, rel[0], rel[2]), (X[2:], 2 * CAP, rel[1], rel[3])]
-        else:
-            flip = (sorted(D + [r]).index(r)) % 2
-            parts = [(X, 0, rel[flip], rel[1 - flip])]
-        ec, es = deal(inside, len(parts)), deal(out if four else inside, len(parts))
-        call(c, "late", [(p[2], ec[i], (L["late"][1], a + p[1], a + p[1] + 2 * CAP), ("rc", 0, 2 * CAP), "r_c")
+        for buf, land, stop, p in ((L["early"][1], "ac", "rd", rel[2]), (L["early"][2], "acs", "rds", rel[3])):
+            sh = deal(out, len(pair))
+            src = {q: (buf, L["early"][3] + CAP * i, L["early"][3] + CAP * i + CAP) for i, q in enumerate(D)}
+            call(c, "early", [(p, inside, src[q], (stop, 0, CAP), "r_d") for q in third]
+                 + [(cores[q], sh[i], src[q], place(land, q, False), "a_ce") for i, q in enumerate(pair)])
+            for q in third:
+                call(p, "r_d", [(cores[q], away(p), (stop, 0, CAP), place(land, q, False), "a_ce")])
+        a, h = L["late"][3], len(X) // 2
+        flip = sorted(D + [r]).index(r) % 2
+        parts = [(X[:h], 0, rel[flip], rel[2 + flip]), (X[h:], h * CAP, rel[1 - flip], rel[3 - flip])]
+        ec, es = deal(inside, 2), deal(out, 2)
+        call(c, "late", [(p[2], ec[i], (L["late"][1], a + p[1], a + p[1] + h * CAP), ("rc", 0, h * CAP), "r_c")
                          for i, p in enumerate(parts)])
-        call(c, "late", [(p[3], es[i], (L["late"][2], a + p[1], a + p[1] + 2 * CAP), ("rcs", 0, 2 * CAP), "r_cs")
+        call(c, "late", [(p[3], es[i], (L["late"][2], a + p[1], a + p[1] + h * CAP), ("rcs", 0, h * CAP), "r_c")
                          for i, p in enumerate(parts)])
         for qs, _, pc, ps in parts:
-            for p, tag, src, land in ((pc, "r_c", "rc", "ac"), (ps, "r_cs", "rcs", "acs")):
+            for p, src, land in ((pc, "rc", "ac"), (ps, "rcs", "acs")):
                 sh = deal(away(p), len(qs))
-                call(p, tag, [(cores[q], sh[i], (src, CAP * i, CAP * i + CAP), place(land, q, True), "a_cl")
-                              for i, q in enumerate(qs)])
+                call(p, "r_c", [(cores[q], sh[i], (src, CAP * i, CAP * i + CAP), place(land, q, True), "a_cl")
+                                for i, q in enumerate(qs)])
 
-        ways = [((r + 1) % N, "ml", "mls", "a_ml", 0), ((r - 1) % N, "mr", "mrs", "a_mr", 1)]
-        over = [w for w in ways if w[0] in X]
-        here = [w for w in ways if w[0] in D]
-        if over:
-            sh = deal(every, len(over))
-            for b in ((0, 1) if four else (1, 0)):
-                s, l, sem = (("qm", "rm", "r_m"), ("qms", "rms", "r_ms"))[b]
-                via = [rel[w[4] + (2 * b if four else 0)] for w in over]
-                call(c, "m", [(p, sh[i], (s, 0, S), (l, 0, S), sem) for i, p in enumerate(via)])
-                for p, w in zip(via, over):
-                    call(p, sem, [(cores[w[0]], away(p), (l, 0, S), (w[1 + b], 0, S), w[3])])
-        if here:
-            sh = deal(out, len(here))
-            for b in (0, 1):
-                call(c, "m", [(cores[w[0]], sh[i], (("qm", "qms")[b], 0, S), (w[1 + b], 0, S), w[3])
-                              for i, w in enumerate(here)])
-    return direct, cross, lay, calls, due
+        wq = max(L["wl"], MIN)
+        for k, (tag, bufs, a, w, stop, sem) in enumerate(
+                (("me", ("nb", "nbs"), OWN_AT, L["we"], ("re", "res"), "r_e"),
+                 ("ml", ("ql", "qls"), wq - L["wl"], L["wl"], ("rm", "rms"), "r_m"))):
+            over = [(i, v) for i, v in enumerate(ways) if v[0] in X]
+            here = [(i, v) for i, v in enumerate(ways) if v[0] in D]
+
+            def land(b, v):
+                at = landing(L, v[1])[k]
+                return (("nb", "nbs")[b], at, at + w), "a_" + v[2] + "el"[k]
+
+            for some in (over, here):
+                for b in (0, 1):
+                    if some:
+                        sh = deal(every, len(some))
+                        call(c, tag, [(rel[i + 2 * b], sh[j], (bufs[b], a, a + w), (stop[b], 0, w), sem)
+                                      for j, (i, v) in enumerate(some)])
+                        for i, v in some:
+                            p = rel[i + 2 * b]
+                            call(p, sem, [(cores[v[0]], away(p), (stop[b], 0, w)) + land(b, v)])
+    return direct, cross, pos, lay, calls, due
 
 
 def rank_program(g, core, T, topo):
-    direct, cross, lay, calls, due = make_plan(T.cores, topo)
+    direct, cross, pos, lay, calls, due = make_plan(T.cores, topo)
     mine = calls.get(core)
     if mine is None:
         return
@@ -221,42 +272,92 @@ def rank_program(g, core, T, topo):
 
     vec, act, ten, syn = g.vector, g.scalar, g.tensor, g.sync
     L, D, X = lay[r], direct[r], cross[r]
-    copy = ActivationFunctionType.Copy
+    copy, ident = ActivationFunctionType.Copy, ActivationFunctionType.Identity
     add, mult = AluOpType.add, AluOpType.mult
 
-    for k in range(8):
-        inc((syn if k < 4 else act).dma_start(T["wl"][16 * k:16 * k + 16, :], T.want[:]), "ldw", 16)
+    def move(q, dst, src, ev):
+        inc(q.tensor_copy(dst, src) if q is vec else q.activation(dst, src, copy), ev)
+
+    for k in range(4):
+        inc((syn if k < 2 else act).dma_start(T["wl"][16 * k:16 * k + 16, :], T.want[:]), "ldw", 16)
+    for k in range(2):
+        inc(act.dma_start(T["ls"][16 * k:16 * k + 16, 0:KS], T.own[:]), "ldl", 16)
+        inc(syn.dma_start(T["ls"][16 * k:16 * k + 16, KS:2 * KS], T.slot[:]), "ldl", 16)
     inc(syn.dma_start(T["xs"][:], T.x[:]), "ldx", 16)
-    for k in range(8):
-        inc(act.dma_start(T["ol"][16 * k:16 * k + 16, :], T.own[:]), "ldo", 16)
-    for k in range(8):
-        inc(syn.dma_start(T["sl"][16 * k:16 * k + 16, :], T.slot[:]), "lds", 16)
+    wait(syn, "a_li")
     inc(syn.dma_start(T["wt"][:], T.w[:]), "ldwt", 16)
 
-    inc(vec.memset(T["half"][:], 0.5), "half")
+    inc(g.iota(T["cnt"][:, 0:128], [[1, 128]], 0, 0, allow_small_or_imprecise_dtypes=True), "io0")
+    inc(g.iota(T["pcol"][:], [[1, 1]], 0, 1, allow_small_or_imprecise_dtypes=True), "io1")
+    inc(g.iota(T["m0"][:], [[1, 16]], 128, -1), "io2")
+    inc(vec.memset(T["diag"][:], 0.0), "z0")
+    inc(vec.memset(T["keep"][:], 1.0), "z1")
+    inc(vec.memset(T["rrow"][:], 0.0), "z2")
     if L["pad"]:
         inc(vec.memset(T["ga"][:, 0:4 * L["pad"]], 0.0), "pad")
-    wait(g, "half")
-    inc(g.affine_select(T["idt"][:], T["half"][:], [[-1, 128]], AluOpType.is_equal, 0.0, 0, 1), "idt")
+        inc(vec.memset(T["mt"][:, 4 * F_W:4 * (F_W + 32)], 0.0), "pad")
+    wait(vec, "z1")
+    inc(vec.memset(T["keep"][:, 0:F_W:16], 0.0), "z2")
+    wait(vec, "z0", "io0", "io1", "io2")
+    inc(vec.tensor_scalar(T["diag"][:, 3:515:4], T["cnt"][:, 0:128], T["pcol"][:], 0.5, AluOpType.is_equal, mult), "diag")
+    inc(vec.tensor_scalar(T["m1"][:], T["m0"][:], 15, None, AluOpType.bitwise_and), "m1")
+    wait(act, "io0")
+    for k in range(1, T_COLS // 128):
+        inc(act.activation(T["cnt"][:, 128 * k:128 * k + 128], T["cnt"][:, 0:128], ident, bias=float(128 * k)), "cnt")
+
     wait(vec, "ldw")
-    inc(vec.tensor_scalar(T["wu"][:], T["wl"][:], 0.0, 4.0, AluOpType.max, mult), "wu")
+    for h in (0, 64):
+        inc(vec.tensor_scalar(T["wu"][h:h + 64, :], T["wl"][0:64, :], 0.0, 4.0, AluOpType.max, mult), "wu")
     wait(g, "wu")
     send_all("list")
-    inc(vec.tensor_scalar(T["su"][:, 0:K], T["wl"][:, K * r:K * r + K], 0.0, 4.0, AluOpType.max, mult), "su")
-    inc(vec.memset(T["e4"][:], 0.0), "e0")
-    wait(vec, "e0", "idt")
-    for b in range(4):
-        inc(vec.tensor_copy(T["e4"][:, 512 * b + b:512 * b + 512:4], T["idt"][:]), "e1")
-    wait(vec, "e1")
-    inc(vec.quantize_mx(T["qe"][:], T["qes"][:], T["e4"][:]), "qe")
-    wait(vec, "ldo")
-    inc(vec.tensor_scalar(T["ou"][:], T["ol"][:], 4.0, None, mult), "ou")
+    wait(vec, "m1")
+    inc(vec.tensor_scalar(T["m16"][:], T["m1"][:], 0.0, None, AluOpType.is_equal), "m16")
+    wait(vec, "wu")
+    inc(vec.tensor_copy(T["su"][:, 0:K], T["wu"][:, K * r:K * r + K]), "su")
+
+    wait(vec, "ldl")
+    inc(vec.tensor_copy(T["ls"][32:64, :], T["ls"][0:32, :]), "d1")
+    wait(vec, "d1")
+    inc(vec.tensor_copy(T["ls"][64:128, :], T["ls"][0:64, :]), "d2")
+    wait(vec, "d2")
+    own, slot = T["ls"][:, 0:KS], T["ls"][:, KS:2 * KS]
+    inc(vec.tensor_copy(T["ou"][:], own), "ou")
+    inc(vec.tensor_scalar(T["t0"][:], slot, 15, None, AluOpType.bitwise_and), "s1")
+    terms = []
+    for (j, d), tmp in zip(jumps(pos), ("t1", "t2", "t3")):
+        inc(vec.tensor_scalar(T[tmp][:], slot, float(CAP * j), float(CAP * d), AluOpType.is_ge, mult), "s1")
+        terms.append(tmp)
+    wait(vec, "s1")
+    inc(vec.tensor_copy(T["sm"][:], T["t0"][:]), "sm")
+    acc = slot
+    for tmp, to, ev in zip(terms, ("t4", "t5", "t6"), ("s2", "s3", "s4")):
+        inc(vec.tensor_tensor(T[to][:], acc, T[tmp][:], add), ev)
+        wait(vec, ev)
+        acc = T[to][:]
+    inc(vec.tensor_scalar(T["so"][:], acc, float(CAP * pos[0]), None, add), "so")
+    wait(g, "so")
+    send_all("slot")
+    wait(act, "cnt", "ou")
+    move(act, T["orow"][:], T["cnt"][:, 0:T_COLS].indirect(T["ou"][:, 0:KS]), "orow")
+    wait(vec, "orow", "sm", "m16")
+    inc(vec.tensor_tensor(T["omask"][:], T["m16"][:, 0:16].indirect(T["sm"][:, 0:KS]), T["orow"][:], mult), "omask")
+    wait(vec, "omask", "so", "z2")
+    move(vec, T["rrow"][:, 0:F_W].indirect(T["so"][:, 0:KS]), T["omask"][:], "rrow")
+    wait(vec, "rrow")
+    inc(vec.tensor_tensor_scan(T["rsum"][:], T["keep"][:], T["rrow"][:], 0.0, mult, add), "rsum")
+    wait(vec, "rsum")
+    inc(vec.tensor_scalar(T["oo"][:], T["rsum"][:, 15:F_W:16], 4.0, None, mult), "oo")
 
     def gather(q, tile, a, n, off, t, name):
-        dst = T[tile][:, 4 * a + t:4 * (a + n):4]
-        src = T["xs"][:, t:W4].indirect(T[off][:, 0:n // 16])
-        inc(q.tensor_copy(dst, src) if q is vec else q.activation(dst, src, copy), name)
+        move(q, T[tile][:, 4 * a + t:4 * (a + n):4], T["xs"][:, t:W4].indirect(T[off][:, 0:n // 16]), name)
 
+    def halve(jobs):
+        for a, n, t, ev in jobs:
+            inc(act.activation(T["oh"][:, F_W * t + a:F_W * t + a + n], T["xs"][:, t:W4].indirect(T["oo"][:, a // 16:(a + n) // 16]),
+                               copy, scale=0.5), ev)
+
+    jobs = [(L["e0"], L["we"], t, "ohe") for t in range(4)] + [(L["l0"], L["wl"], t, "ohl") for t in range(4)]
+    first = 2 * S // L["we"]
     wait(act, "su", "ldx")
     for t in range(4):
         gather(act, "ga", L["self"], CAP, "su", t, "gs")
@@ -277,84 +378,99 @@ def rank_program(g, core, T, topo):
         inc(vec.quantize_mx(T[part[1]][:, 0:w], T[part[2]][:, 0:w], T[part[0]][:, 0:4 * w]), qev)
         wait(g, qev)
         send_all("early" if ev == "ge" else "late")
-
-    wait(act, "ou")
-    for t in range(4):
-        inc(act.activation(T["oh"][:, S * t:S * t + S], T["xs"][:, t:W4].indirect(T["ou"][:, 0:S // 16]), copy, scale=0.5), "oh")
-    order = sorted(D + [r]) if L["early_is_x"] else X
-    order = order + [q for q in range(N) if q not in order]
-    pos = [order.index(q) for q in range(N)]
-    steps = [(j, pos[j] - pos[j - 1] - 1) for j in range(1, N) if pos[j] - pos[j - 1] != 1]
-    wait(vec, "lds")
-    terms = []
-    for (j, d), tmp in zip(steps, ("ta", "tb", "tc")):
-        inc(vec.tensor_scalar(T[tmp][:], T["sl"][:], float(CAP * j), float(CAP * d), AluOpType.is_ge, mult), "s1")
-        terms.append(tmp)
-    wait(vec, "ldwt")
-    inc(vec.quantize_mx(T["wq"][:], T["wqs"][:], T["wt"][:]), "wq")
-    wait(vec, "s1")
-    acc = "sl"
-    for tmp, to, ev in zip(terms, ("td", "te", "tf"), ("s2", "s3", "s4")):
-        inc(vec.tensor_tensor(T[to][:], T[acc][:], T[tmp][:], add), ev)
-        wait(vec, ev)
-        acc = to
-    inc(vec.tensor_copy(T["so"][:], T[acc][:]), "s5")
-
-    lo, hi = min(L["self"], L["lin"] - 128), L["lin"]
-    wait(ten, "qe", "qlate" if L["early_is_x"] else "qearly", "a_ce")
+        if ev == "ge":
+            wait(act, "oo")
+            halve(jobs[:first])
+        else:
+            halve(jobs[first:])
+    wait(vec, "diag")
     for b in range(4):
-        inc(ten.matmul_mx(T["pe"][:, 512 * b:512 * b + hi - lo], T["qe"][:, 128 * b:128 * b + 128], T["qes"][:, 128 * b:128 * b + 128],
-                          T["ac"][:, lo:hi], T["acs"][:, lo:hi], True, True), "me%d" % b)
+        inc(vec.quantize_mx(T["qe"][:, 128 * b:128 * b + 128], T["qes"][:, 128 * b:128 * b + 128], T["diag"][:, 3 - b:515 - b]), "qe")
+
+    def unpack(ps, lo, hi, ev):
+        for b in range(4):
+            inc(ten.matmul_mx(T[ps][:, 512 * b:512 * b + hi - lo], T["qe"][:, 128 * b:128 * b + 128],
+                              T["qes"][:, 128 * b:128 * b + 128], T["ac"][:, lo:hi], T["acs"][:, lo:hi], True, True), ev % b)
+
+    def sums(ps, runs, ev, done):
+        for b in range(4):
+            wait(vec, ev % b)
+            for a, f, n in runs:
+                inc(vec.tensor_tensor(T["mt"][:, 4 * f + b:4 * (f + n):4], T[ps][:, 512 * b + a:512 * b + a + n],
+                                      T["oh"][:, F_W * b + f:F_W * b + f + n], add), done)
+        wait(vec, done)
+
+    lo, hi = min(L["self"], L["lin"] - MIN), L["lin"]
+    wait(ten, "qe", "qlate" if L["early_is_x"] else "qearly", "a_ce")
+    unpack("pe", lo, hi, "me%d")
     runs = []
     for q, a in sorted([(r, L["self"])] + [(q, L["ein"] + CAP * i) for i, q in enumerate(D)], key=lambda v: pos[v[0]]):
-        if runs and runs[-1][0] + runs[-1][2] == a - lo and runs[-1][1] + runs[-1][2] == CAP * pos[q]:
+        if runs and runs[-1][0] + runs[-1][2] == a - lo:
             runs[-1][2] += CAP
         else:
             runs.append([a - lo, CAP * pos[q], CAP])
-
-    def unpack(q, ps, b, a, f, n, ev):
-        dst, src = T["ft"][:, F_W * b + f:F_W * b + f + n], T[ps][:, 512 * b + a:512 * b + a + n]
-        inc(q.tensor_copy(dst, src) if q is vec else q.activation(dst, src, copy), ev)
-
-    for b in range(4):
-        q = vec if b < 2 else act
-        wait(q, "me%d" % b)
-        for a, f, n in runs:
-            unpack(q, "pe", b, a, f, n, "fe")
+    wait(vec, "ohe")
+    sums("pe", runs, "me%d", "mae")
+    we, wl = max(L["we"], MIN), max(L["wl"], MIN)
+    inc(vec.quantize_mx(T["nb"][:, OWN_AT:OWN_AT + we], T["nbs"][:, OWN_AT:OWN_AT + we],
+                        T["mt"][:, 4 * L["e0"]:4 * (L["e0"] + we)]), "mqe")
+    wait(g, "mqe")
+    send_all("me")
 
     end = L["lin"] + L["nl"]
-    lo = min(L["lin"], end - 128)
     wait(ten, "a_cl")
-    for b in range(4):
-        inc(ten.matmul_mx(T["pl"][:, 512 * b:512 * b + end - lo], T["qe"][:, 128 * b:128 * b + 128], T["qes"][:, 128 * b:128 * b + 128],
-                          T["ac"][:, lo:end], T["acs"][:, lo:end], True, True), "mlt%d" % b)
-    for b in range(4):
-        q = vec if b == 0 else act
-        wait(q, "mlt%d" % b)
-        unpack(q, "pl", b, L["lin"] - lo, CAP * pos[X[0]], L["nl"], "fl%d" % b)
-    wait(vec, "fe", "s5", "oh")
-    for b in range(4):
-        wait(vec, "fl%d" % b)
-        inc(vec.tensor_tensor(T["mt"][:, b:4 * S:4], T["ft"][:, F_W * b:F_W * b + F_W].indirect(T["so"][:, 0:S // 16]),
-                              T["oh"][:, S * b:S * b + S], add), "ma")
-    wait(vec, "ma")
-    inc(vec.quantize_mx(T["qm"][:], T["qms"][:], T["mt"][:]), "mq")
-    wait(g, "mq")
-    send_all("m")
+    unpack("pl", end - wl, end, "ml%d")
+    wait(vec, "ohl")
+    sums("pl", [[wl - L["wl"], L["l0"], L["wl"]]], "ml%d", "mal")
+    a = L["l0"] + L["wl"] - wl
+    inc(vec.quantize_mx(T["ql"][:, 0:wl], T["qls"][:, 0:wl], T["mt"][:, 4 * a:4 * (a + wl)]), "mql")
+    wait(g, "mql")
+    send_all("ml")
+    wait(vec, "ldwt")
+    inc(vec.quantize_mx(T["wq"][:], T["wqs"][:], T["wt"][:]), "wq")
 
-    sides = [(0, "ml", "mls", "a_ml", (r - 1) % N), (2, "mr", "mrs", "a_mr", (r + 1) % N)]
-    sides.sort(key=lambda v: v[4] in X)
-    wait(ten, "wq", "fe", "mq")
-    for i, buf, pl, sem, _ in [(1, "qm", "qms", None, r)] + sides:
-        if sem:
-            wait(ten, sem)
-        inc(ten.matmul_mx(T["pe"][:, 512 * i:512 * i + S], T["wq"][:], T["wqs"][:], T[buf][:], T[pl][:], True, True), "y%d" % i)
-        q, dq = (act, act) if i == 2 else (vec, syn)
-        wait(q, "y%d" % i)
-        dst, src = T["yb"][:, S * i:S * i + S], T["pe"][:, 512 * i:512 * i + S]
-        inc(q.tensor_copy(dst, src) if q is vec else q.activation(dst, src, copy), "yc%d" % i)
-        wait(dq, "yc%d" % i)
-        inc(dq.dma_start(T.y[:, S * i:S * i + S], dst), "yst", 16)
+    def product(ps, bank, buf, a, n, w, ev):
+        inc(ten.matmul_mx(T[ps][:, 512 * bank:512 * bank + w], T["wq"][:], T["wqs"][:], T[buf][:, a:a + w], T[buf + "s"][:, a:a + w],
+                          True, True), ev)
+
+    def pick(q, i, off, a, n):
+        move(q, T["yb"][:, S * i + a:S * i + a + n], T["yt%d" % i][:, 0:F_W].indirect(T[off][:, a // 16:(a + n) // 16]), "yg%d" % i)
+
+    def store(q, i):
+        wait(q, "yg%d" % i)
+        inc(q.dma_start(T.y[:, S * i:S * i + S], T["yb"][:, S * i:S * i + S]), "yst", 16)
+
+    wait(ten, "wq", "mqe", "mql")
+    product("pe", 0, "nb", OWN_AT, L["we"], we, "ye1")
+    product("pe", 1, "ql", 0, L["wl"], wl, "yl1")
+    wait(act, "ye1")
+    move(act, T["yt1"][:, L["e0"]:L["e0"] + L["we"]], T["pe"][:, 0:L["we"]], "ce1")
+    wait(act, "yl1")
+    move(act, T["yt1"][:, L["l0"]:L["l0"] + L["wl"]], T["pe"][:, 512 + wl - L["wl"]:512 + wl], "cl1")
+    wait(act, "ce1", "cl1")
+    pick(act, 1, "so", 0, S)
+    store(syn, 1)
+
+    sides = sorted([(0, "l", (r - 1) % N), (2, "r", (r + 1) % N)], key=lambda v: v[2] in X)
+    alike = (sides[0][2] in X) == (sides[1][2] in X)
+    for k, (ps, ev, cev) in enumerate((("pe", "ye%d", "ce%d"), ("pl", "yl%d", "cl%d"))):
+        for j, (i, n, q) in enumerate(sides):
+            Q = lay[q]
+            at, f, w = landing(Q, i)[k], Q[("e0", "l0")[k]], Q[("we", "wl")[k]]
+            wide = max(w, MIN)
+            skip = wide - w if i == 2 else 0
+            bank = 2 * (1 - k) + j
+            wait(ten, "a_" + n + "el"[k])
+            product(ps, bank, "nb", at - skip, w, wide, ev % i)
+            eng = vec if k == 0 or j == 1 else act
+            wait(eng, ev % i)
+            move(eng, T["yt%d" % i][:, f:f + w], T[ps][:, 512 * bank + skip:512 * bank + skip + w], cev % i)
+            if k == 1:
+                shares = [(eng, 0, S)] if alike or j == 0 else [(vec, 0, S // 2), (act, S // 2, S // 2)]
+                for e, a, m in shares:
+                    wait(e, "ce%d" % i, "cl%d" % i, "a_s" + n)
+                    pick(e, i, "s" + n, a, m)
+                store(act if eng is act else syn, i)
     wait(g, "yst", "sent")
     for name in count:
         if name not in waited:

@@ -7,7 +7,13 @@ KS = S // 16
 W4 = 4 * T_COLS
 F_W = N * CAP
 MIN = 128
-OWN_AT, RIGHT_AT, NB_W = F_W, F_W + S, 2 * F_W + S
+HALF = 2 * CAP
+PAD = MIN - HALF
+CHUNKS = F_W // HALF
+OWN_AT = F_W + PAD
+RIGHT_AT = OWN_AT + S + PAD
+NB_W = RIGHT_AT + F_W
+AC_W = 2 * MIN + S + CAP + 2 * HALF
 
 X4, U8 = "float8_e4m3fn_x4", "uint8"
 SCRATCH = {
@@ -43,59 +49,55 @@ SCRATCH = {
     "sl": ("sbuf", [128, KS], "uint16"),
     "sr": ("sbuf", [128, KS], "uint16"),
     "diag": ("sbuf", [128, 516], "bfloat16"),
-    "qe": ("sbuf", [128, 512], X4),
-    "qes": ("sbuf", [128, 512], U8),
+    "qe": ("sbuf", [128, 4 * MIN], X4),
+    "qes": ("sbuf", [128, 4 * MIN], U8),
+    "qx": ("sbuf", [128, 2 * MIN], X4),
+    "qxs": ("sbuf", [128, 2 * MIN], U8),
     "wq": ("sbuf", [128, 128], X4),
     "wqs": ("sbuf", [128, 128], U8),
-    "ga": ("sbuf", [128, 4 * 144], "bfloat16"),
-    "gx": ("sbuf", [128, 4 * 192], "bfloat16"),
-    "ac": ("sbuf", [128, 384], X4),
-    "acs": ("sbuf", [128, 384], U8),
-    "qx": ("sbuf", [128, 192], X4),
-    "qxs": ("sbuf", [128, 192], U8),
+    "ga": ("sbuf", [128, 4 * S], "bfloat16"),
+    "gx": ("sbuf", [128, 4 * 2 * MIN], "bfloat16"),
+    "ac": ("sbuf", [128, AC_W], X4),
+    "acs": ("sbuf", [128, AC_W], U8),
     "oh": ("sbuf", [128, 4 * F_W], "bfloat16"),
-    "mt": ("sbuf", [128, 4 * (F_W + 32)], "bfloat16"),
+    "mt": ("sbuf", [128, 4 * (F_W + 2 * PAD)], "bfloat16"),
     "nb": ("sbuf", [128, NB_W], X4),
     "nbs": ("sbuf", [128, NB_W], U8),
-    "ql": ("sbuf", [128, S], X4),
-    "qls": ("sbuf", [128, S], U8),
+    "ql": ("sbuf", [128, 2 * MIN], X4),
+    "qls": ("sbuf", [128, 2 * MIN], U8),
     "yt0": ("sbuf", [128, F_W], "float32"),
     "yt1": ("sbuf", [128, F_W], "float32"),
     "yt2": ("sbuf", [128, F_W], "float32"),
     "yb": ("sbuf", [128, 3 * S], "float32"),
-    "rl": ("sbuf", [128, K], "uint16"),
+    "rl": ("sbuf", [128, K * N], "uint16"),
     "rs": ("sbuf", [128, KS], "uint16"),
-    "rc": ("sbuf", [128, 2 * CAP], X4),
-    "rcs": ("sbuf", [128, 2 * CAP], U8),
+    "rc": ("sbuf", [128, HALF], X4),
+    "rcs": ("sbuf", [128, 4 * HALF], U8),
     "rd": ("sbuf", [128, CAP], X4),
-    "rds": ("sbuf", [128, CAP], U8),
-    "re": ("sbuf", [128, S], X4),
-    "res": ("sbuf", [128, S], U8),
-    "rm": ("sbuf", [128, S], X4),
+    "rds": ("sbuf", [128, 4 * CAP], U8),
+    "ra": ("sbuf", [128, S], X4),
+    "ras": ("sbuf", [128, S], U8),
+    "rm": ("sbuf", [128, HALF], X4),
     "rms": ("sbuf", [128, S], U8),
     "pe": ("psum", [128, 2048], "float32"),
     "pl": ("psum", [128, 2048], "float32"),
 }
 CODES = {k for k, v in SCRATCH.items() if v[2] == X4}
-ARRIVALS = ["a_li", "a_lj", "a_sl", "a_sr", "a_ce", "a_cl", "a_le", "a_re", "a_ll", "a_rl", "r_l", "r_s", "r_d", "r_c", "r_e", "r_m"]
+ARRIVALS = ["a_li", "a_l0", "a_l1", "a_sl", "a_sr", "a_c0", "a_c1", "a_c2", "a_le", "a_re", "a_ll", "a_rl",
+            "r_l", "r_s", "r_d", "r_c", "r_a", "r_as", "r_m", "r_ms"]
 EVENTS = (["ldw", "ldx", "ldl", "ldwt", "z0", "z1", "z2", "pad", "io0", "io1", "io2", "cnt", "diag", "m1", "m16", "wu", "su",
-           "d1", "d2", "ou", "s1", "s2", "s3", "s4", "s5", "so", "sm", "orow", "omask", "rrow", "rsum", "oo", "qe", "gs", "ge",
-           "qearly", "gl", "qlate", "ohe", "ohl", "wq", "mae", "mal", "mqe", "mql", "yst", "sent"]
-          + ["me%d" % b for b in range(4)] + ["ml%d" % b for b in range(4)]
+           "d1", "d2", "ou", "s1", "s2", "s3", "s4", "so", "sm", "orow", "omask", "rrow", "rsum", "oo", "qe", "gs",
+           "wq", "yst", "sent"]
+          + [s + t for s in "gq" for t in ("early", "late0", "late1")]
+          + [s % k for s in ("ma%d", "mq%d", "oh%d") for k in range(CHUNKS)]
+          + ["un%d%d" % (k, b) for k in range(CHUNKS) for b in range(4)]
           + [s % i for s in ("ye%d", "yl%d", "ce%d", "cl%d", "yg%d") for i in range(3)])
 SEMAPHORES = ARRIVALS + EVENTS
 
 
-def deal(engines, k, back=False):
-    n = len(engines)
-    sizes = [n // 2, n // 4, n // 4] if k == 3 else [n // k] * k
-    if back:
-        sizes = sizes[::-1]
-    out, a = [], 0
-    for s in sizes:
-        out.append(engines[a:a + s])
-        a += s
-    return out
+def deal(engines, k):
+    n = len(engines) // k
+    return [engines[i * n:i * n + n] for i in range(k)]
 
 
 def orders(items):
@@ -119,18 +121,25 @@ def groups(cores, topo):
 
 
 def layout(r, direct, cross, pos):
-    A, X = ("ga", "ac", "acs"), ("gx", "qx", "qxs")
     ne, nl = CAP * len(direct[r]), CAP * len(cross[r])
-    if ne >= MIN:
-        na, nx, pad = nl + CAP, ne, 0
-        early, late, me = X + (0,), A + (0,), nl
-    else:
-        na, nx = MIN, nl
-        pad = na - CAP - ne
-        early, late, me = A + (pad,), X + (0,), pad + ne
-    return {"na": na, "nx": nx, "pad": pad, "early": early, "late": late, "self": me, "ein": na, "lin": na + ne,
-            "ne": ne, "nl": nl, "early_is_x": ne >= MIN,
-            "e0": CAP * min(pos[q] for q in direct[r] + [r]), "we": ne + CAP, "l0": CAP * pos[cross[r][0]], "wl": nl}
+    na = max(ne + CAP, MIN)
+    pad, wide = na - CAP - ne, ne > nl
+    at = 2 * MIN if wide else HALF
+    mine = pos[r] // 2
+    rest = [k for k in range(CHUNKS) if k != mine]
+    base = {rest[0]: at + na + CAP, rest[1]: at + na + CAP + HALF if wide else 0}
+    col = [base[pos[q] // 2] + CAP * (pos[q] % 2) if pos[q] // 2 != mine else at + na - CAP * (q == r) for q in range(N)]
+    early = [k for k in [mine] + rest if any(pos[q] // 2 == k for q in direct[r])]
+    late = [k for k in (rest if pos[r] % 2 == 0 else rest[::-1]) if k not in early]
+    h = len(cross[r]) // 2
+    serve = [cross[r][:h], cross[r][h:]]
+    if wide and pos[serve[0][0]] % 2 != mine:
+        serve = serve[::-1]
+    if not wide:
+        serve.sort(key=lambda some: -sum((q + d) % N in cross[q] for q in some for d in (1, -1)))
+    return {"serve": serve, "xbuf": "ac" if wide else "qx", "xw": h * CAP, "na": na, "pad": pad, "at": at, "wide": wide, "col": col,
+            "ne": ne, "early": early, "late": late,
+            "e0": HALF * min(early), "we": HALF * len(early), "l0": HALF * min(late), "wl": HALF * len(late)}
 
 
 def landing(L, side):
@@ -143,7 +152,8 @@ def make_plan(cores, topo):
     calls, due = {}, {}
 
     def call(core, tag, trs):
-        calls.setdefault(core, []).append((tag, trs))
+        if trs:
+            calls.setdefault(core, []).append((tag, trs))
         for to, eng, src, dst, sem in trs:
             due[(to, sem)] = due.get((to, sem), 0) + len(eng)
 
@@ -162,69 +172,79 @@ def make_plan(cores, topo):
         def away(p):
             return topo.engines(p, cores[X[0]])
 
-        sh = deal(inside, len(X))
-        call(c, "list", [(rel[i], sh[i], ("wu", K * q, K * q + K), ("rl", 0, K), "r_l") for i, q in enumerate(X)])
+        h, sh = len(X) // 2, deal(inside, 2)
+        asked = sorted(enumerate(X), key=lambda v: r in lay[v[1]]["serve"][1])
+        for n in range(h):
+            call(c, "list", [(rel[i], sh[m], ("wu", K * q, K * q + K), ("rl", 0, K), "r_l")
+                             for m, (i, q) in enumerate(asked[2 * n:2 * n + 2])])
         for i, q in enumerate(X):
-            j = cross[q].index(r)
-            call(rel[i], "r_l", [(cores[q], away(rel[i]), ("rl", 0, K), ("lj", K * j, K * j + K), "a_lj")])
-        plane = sorted(D + [r])
-        third = [plane[(plane.index(r) + 2) % len(plane)]] if len(D) > 2 else []
-        pair = [q for q in D if q not in third]
+            a = [2 * K * n + K * some.index(r) for n, some in enumerate(lay[q]["serve"]) if r in some][0]
+            call(rel[i], "r_l", [(cores[q], away(rel[i]), ("rl", 0, K), ("lj", a, a + K), "a_l%d" % (a // (2 * K)))])
+        third = [q for q in D if (pos[q] - pos[r]) % (len(D) + 1) == 2]
+        pair = sorted((q for q in D if q not in third), key=lambda q: pos[q] // 2 != pos[r] // 2)
         for some in (pair, third):
-            if some:
-                sh = deal(out, len(some))
-                call(c, "list", [(cores[q], sh[i], ("wu", K * q, K * q + K),
-                                  ("li", K * direct[q].index(r), K * direct[q].index(r) + K), "a_li") for i, q in enumerate(some)])
+            sh = deal(out, max(len(some), 1))
+            call(c, "list", [(cores[q], sh[i], ("wu", K * q, K * q + K),
+                              ("li", K * direct[q].index(r), K * direct[q].index(r) + K), "a_li") for i, q in enumerate(some)])
         sh = deal(inside, 2)
         call(c, "slot", [(rel[3 - i], sh[i], ("so", 0, KS), ("rs", 0, KS), "r_s") for i in range(2)])
         for i, (q, side, n) in enumerate(ways):
             call(rel[3 - i], "r_s", [(cores[q], away(rel[3 - i]), ("rs", 0, KS), ("s" + n, 0, KS), "a_s" + n)])
 
-        def place(buf, q, late):
-            a = lay[q]["lin"] + CAP * cross[q].index(r) if late else lay[q]["ein"] + CAP * direct[q].index(r)
+        def place(buf, q):
+            return (buf, lay[q]["col"][r], lay[q]["col"][r] + CAP), "a_c%d" % (pos[r] // 2)
+
+        def source(buf, q):
+            a = L["at"] + L["pad"] + CAP * D.index(q)
             return (buf, a, a + CAP)
 
-        for buf, land, stop, p in ((L["early"][1], "ac", "rd", rel[2]), (L["early"][2], "acs", "rds", rel[3])):
-            sh = deal(out, len(pair))
-            src = {q: (buf, L["early"][3] + CAP * i, L["early"][3] + CAP * i + CAP) for i, q in enumerate(D)}
-            call(c, "early", [(p, inside, src[q], (stop, 0, CAP), "r_d") for q in third]
-                 + [(cores[q], sh[i], src[q], place(land, q, False), "a_ce") for i, q in enumerate(pair)])
-            for q in third:
-                call(p, "r_d", [(cores[q], away(p), (stop, 0, CAP), place(land, q, False), "a_ce")])
-        a, h = L["late"][3], len(X) // 2
-        flip = sorted(D + [r]).index(r) % 2
-        parts = [(X[:h], 0, rel[flip], rel[2 + flip]), (X[h:], h * CAP, rel[1 - flip], rel[3 - flip])]
-        ec, es = deal(inside, 2), deal(out, 2)
-        call(c, "late", [(p[2], ec[i], (L["late"][1], a + p[1], a + p[1] + h * CAP), ("rc", 0, h * CAP), "r_c")
-                         for i, p in enumerate(parts)])
-        call(c, "late", [(p[3], es[i], (L["late"][2], a + p[1], a + p[1] + h * CAP), ("rcs", 0, h * CAP), "r_c")
-                         for i, p in enumerate(parts)])
-        for qs, _, pc, ps in parts:
-            for p, src, land in ((pc, "rc", "ac"), (ps, "rcs", "acs")):
-                sh = deal(away(p), len(qs))
-                call(p, "r_c", [(cores[q], sh[i], (src, CAP * i, CAP * i + CAP), place(land, q, True), "a_cl")
-                                for i, q in enumerate(qs)])
+        for b, (buf, stop) in enumerate((("ac", "rd"), ("acs", "rds"))):
+            some = [(v, rel[2 * n + (b + n) % 2]) for n, v in enumerate(pair[1:] + third)]
+            call(c, "early", [(p, deal(inside, 2)[n], source(buf, v), (stop, 0, CAP), "r_d") for n, (v, p) in enumerate(some)]
+                 + [(cores[pair[0]], out, source(buf, pair[0])) + place(buf, pair[0])])
+            for v, p in some:
+                call(p, "r_d", [(cores[v], away(p), (stop, 0, CAP)) + place(buf, v)])
+        j, w = pos[r], L["xw"]
+        for n, some in enumerate(L["serve"]):
+            a = MIN - n * w
+            if L["wide"]:
+                ps = [rel[2 * b + (j + n) % 2] for b in (0, 1)]
+                call(c, "late%d" % n, [(ps[0], inside, ("ac", a, a + w), ("rc", 0, w), "r_c"),
+                                       (ps[1], out, ("acs", a, a + 4 * w), ("rcs", 0, 4 * w), "r_c")])
+                for p, stop, land in zip(ps, ("rc", "rcs"), ("ac", "acs")):
+                    call(p, "r_c", [(cores[some[0]], away(p), (stop, 0, CAP)) + place(land, some[0])])
+            elif n == 0:
+                for b, s in enumerate(("", "s")):
+                    ps = [rel[2 * b + (j + m) % 2] for m in range(h)]
+                    call(c, "late0", [(p, deal(every, h)[m], ("qx" + s, a + CAP * m, a + CAP * m + CAP), ("rc" + s, 0, CAP), "r_c")
+                                      for m, p in enumerate(ps)])
+                    for p, q in zip(ps, some):
+                        call(p, "r_c", [(cores[q], away(p), ("rc" + s, 0, CAP)) + place("ac" + s, q)])
+            else:
+                for m, q in enumerate(some):
+                    ps, at = [rel[2 * b + (j + m) % 2] for b in (0, 1)], a + CAP * m
+                    lo = min(at, 2 * MIN - 4 * CAP)
+                    call(c, "late1", [(ps[0], inside, ("qx", at, at + CAP), ("rd", 0, CAP), "r_d"),
+                                      (ps[1], out, ("qxs", lo, lo + 4 * CAP), ("rds", 0, 4 * CAP), "r_d")])
+                    call(ps[0], "r_d", [(cores[q], away(ps[0]), ("rd", 0, CAP)) + place("ac", q)])
+                    call(ps[1], "r_d", [(cores[q], away(ps[1]), ("rds", at - lo, at - lo + CAP)) + place("acs", q)])
 
-        wq = max(L["wl"], MIN)
-        for k, (tag, bufs, a, w, stop, sem) in enumerate(
-                (("me", ("nb", "nbs"), OWN_AT, L["we"], ("re", "res"), "r_e"),
-                 ("ml", ("ql", "qls"), wq - L["wl"], L["wl"], ("rm", "rms"), "r_m"))):
-            over = [(i, v) for i, v in enumerate(ways) if v[0] in X]
-            here = [(i, v) for i, v in enumerate(ways) if v[0] in D]
-
-            def land(b, v):
-                at = landing(L, v[1])[k]
-                return (("nb", "nbs")[b], at, at + w), "a_" + v[2] + "el"[k]
-
-            for some in (over, here):
-                for b in (0, 1):
-                    if some:
-                        sh = deal(every, len(some))
-                        call(c, tag, [(rel[i + 2 * b], sh[j], (bufs[b], a, a + w), (stop[b], 0, w), sem)
-                                      for j, (i, v) in enumerate(some)])
-                        for i, v in some:
-                            p = rel[i + 2 * b]
-                            call(p, sem, [(cores[v[0]], away(p), (stop[b], 0, w)) + land(b, v)])
+        last, n = "m%d" % L["early"][-1], len(L["late"])
+        pieces = [(last, "nb", OWN_AT, L["we"], 0, 0, 0, "ra"), (last, "nbs", OWN_AT, L["we"], 0, 0, 1, "ras")]
+        pieces += [("m%d" % m, "ql", PAD, HALF, 1, HALF * m - L["l0"], i, "rm") for i, m in enumerate(L["late"])]
+        pieces += [("m%d" % L["late"][-1], "qls", PAD, L["wl"], 1, 0, n % 2, "rms")]
+        for tag, src, a, w, k, off, by, stop in pieces:
+            straight = k == 1 and all(q in D for q, side, name in ways)
+            sh, sem, trs = deal(out if straight else every, 2), "r_" + stop[1:], []
+            for i, (q, side, name) in enumerate(ways):
+                p, at = rel[i + 2 * by], landing(L, side)[k] + off
+                end = (("nb" if src in CODES else "nbs", at, at + w), "a_" + name + "el"[k])
+                if straight:
+                    trs.append((cores[q], sh[i], (src, a + off, a + off + w)) + end)
+                else:
+                    trs.append((p, sh[i], (src, a + off, a + off + w), (stop, 0, w), sem))
+                    call(p, sem, [(cores[q], away(p), (stop, 0, w)) + end])
+            call(c, tag, trs)
     return direct, cross, pos, lay, calls, due
 
 
@@ -278,6 +298,9 @@ def rank_program(g, core, T, topo):
     def move(q, dst, src, ev):
         inc(q.tensor_copy(dst, src) if q is vec else q.activation(dst, src, copy), ev)
 
+    def quantise(buf, a, tile, b, w, ev):
+        inc(vec.quantize_mx(T[buf][:, a:a + w], T[buf + "s"][:, a:a + w], T[tile][:, 4 * b:4 * (b + w)]), ev)
+
     for k in range(4):
         inc((syn if k < 2 else act).dma_start(T["wl"][16 * k:16 * k + 16, :], T.want[:]), "ldw", 16)
     for k in range(2):
@@ -287,38 +310,41 @@ def rank_program(g, core, T, topo):
     wait(syn, "a_li")
     inc(syn.dma_start(T["wt"][:], T.w[:]), "ldwt", 16)
 
+    inc(g.iota(T["m0"][:], [[1, 16]], 128, -1), "io2")
     inc(g.iota(T["cnt"][:, 0:128], [[1, 128]], 0, 0, allow_small_or_imprecise_dtypes=True), "io0")
     inc(g.iota(T["pcol"][:], [[1, 1]], 0, 1, allow_small_or_imprecise_dtypes=True), "io1")
-    inc(g.iota(T["m0"][:], [[1, 16]], 128, -1), "io2")
     inc(vec.memset(T["diag"][:], 0.0), "z0")
     inc(vec.memset(T["keep"][:], 1.0), "z1")
-    inc(vec.memset(T["rrow"][:], 0.0), "z2")
-    if L["pad"]:
-        inc(vec.memset(T["ga"][:, 0:4 * L["pad"]], 0.0), "pad")
-        inc(vec.memset(T["mt"][:, 4 * F_W:4 * (F_W + 32)], 0.0), "pad")
-    wait(vec, "z1")
+    wait(vec, "z1", "io2")
     inc(vec.memset(T["keep"][:, 0:F_W:16], 0.0), "z2")
-    wait(vec, "z0", "io0", "io1", "io2")
-    inc(vec.tensor_scalar(T["diag"][:, 3:515:4], T["cnt"][:, 0:128], T["pcol"][:], 0.5, AluOpType.is_equal, mult), "diag")
     inc(vec.tensor_scalar(T["m1"][:], T["m0"][:], 15, None, AluOpType.bitwise_and), "m1")
+    wait(vec, "m1")
+    inc(vec.tensor_scalar(T["m16"][:], T["m1"][:], 0.0, None, AluOpType.is_equal), "m16")
     wait(act, "io0")
     for k in range(1, T_COLS // 128):
         inc(act.activation(T["cnt"][:, 128 * k:128 * k + 128], T["cnt"][:, 0:128], ident, bias=float(128 * k)), "cnt")
+    wait(act, "cnt")
+    inc(act.activation(T["rrow"][:], T["cnt"][:, 0:F_W], copy, scale=0.0), "z2")
 
     wait(vec, "ldw")
     for h in (0, 64):
         inc(vec.tensor_scalar(T["wu"][h:h + 64, :], T["wl"][0:64, :], 0.0, 4.0, AluOpType.max, mult), "wu")
     wait(g, "wu")
     send_all("list")
-    wait(vec, "m1")
-    inc(vec.tensor_scalar(T["m16"][:], T["m1"][:], 0.0, None, AluOpType.is_equal), "m16")
-    wait(vec, "wu")
-    inc(vec.tensor_copy(T["su"][:, 0:K], T["wu"][:, K * r:K * r + K]), "su")
+    wait(vec, "z0", "io0", "io1")
+    inc(vec.tensor_scalar(T["diag"][:, 3:515:4], T["cnt"][:, 0:128], T["pcol"][:], 0.5, AluOpType.is_equal, mult), "diag")
+
+    def constant(b):
+        inc(vec.quantize_mx(T["qe"][:, 128 * b:128 * b + 128], T["qes"][:, 128 * b:128 * b + 128], T["diag"][:, 3 - b:515 - b]), "qe")
 
     wait(vec, "ldl")
     inc(vec.tensor_copy(T["ls"][32:64, :], T["ls"][0:32, :]), "d1")
+    wait(vec, "wu")
+    inc(vec.tensor_copy(T["su"][:, 0:K], T["wu"][:, K * r:K * r + K]), "su")
     wait(vec, "d1")
     inc(vec.tensor_copy(T["ls"][64:128, :], T["ls"][0:64, :]), "d2")
+    wait(vec, "diag")
+    constant(0)
     wait(vec, "d2")
     own, slot = T["ls"][:, 0:KS], T["ls"][:, KS:2 * KS]
     inc(vec.tensor_copy(T["ou"][:], own), "ou")
@@ -339,97 +365,97 @@ def rank_program(g, core, T, topo):
     send_all("slot")
     wait(act, "cnt", "ou")
     move(act, T["orow"][:], T["cnt"][:, 0:T_COLS].indirect(T["ou"][:, 0:KS]), "orow")
+    pads = [("mt", 0, PAD), ("mt", PAD + L["e0"] + L["we"], PAD), ("gx", 0, MIN - L["xw"]), ("gx", MIN + L["xw"], MIN - L["xw"])]
+    for buf, a, w in pads + ([("ga", 0, L["pad"])] if L["pad"] else []):
+        inc(act.activation(T[buf][:, 4 * a:4 * (a + w)], T["cnt"][:, 0:4 * w], copy, scale=0.0), "pad")
     wait(vec, "orow", "sm", "m16")
     inc(vec.tensor_tensor(T["omask"][:], T["m16"][:, 0:16].indirect(T["sm"][:, 0:KS]), T["orow"][:], mult), "omask")
+    constant(1)
     wait(vec, "omask", "so", "z2")
     move(vec, T["rrow"][:, 0:F_W].indirect(T["so"][:, 0:KS]), T["omask"][:], "rrow")
+    constant(2)
     wait(vec, "rrow")
     inc(vec.tensor_tensor_scan(T["rsum"][:], T["keep"][:], T["rrow"][:], 0.0, mult, add), "rsum")
+    constant(3)
     wait(vec, "rsum")
     inc(vec.tensor_scalar(T["oo"][:], T["rsum"][:, 15:F_W:16], 4.0, None, mult), "oo")
 
     def gather(q, tile, a, n, off, t, name):
-        move(q, T[tile][:, 4 * a + t:4 * (a + n):4], T["xs"][:, t:W4].indirect(T[off][:, 0:n // 16]), name)
+        move(q, T[tile][:, 4 * a + t:4 * (a + n):4], T["xs"][:, t:W4].indirect(off), name)
 
-    def halve(jobs):
-        for a, n, t, ev in jobs:
-            inc(act.activation(T["oh"][:, F_W * t + a:F_W * t + a + n], T["xs"][:, t:W4].indirect(T["oo"][:, a // 16:(a + n) // 16]),
-                               copy, scale=0.5), ev)
+    def halve(k):
+        a = HALF * k
+        for t in range(4):
+            inc(act.activation(T["oh"][:, F_W * t + a:F_W * t + a + HALF],
+                               T["xs"][:, t:W4].indirect(T["oo"][:, a // 16:(a + HALF) // 16]), copy, scale=0.5), "oh%d" % k)
 
-    jobs = [(L["e0"], L["we"], t, "ohe") for t in range(4)] + [(L["l0"], L["wl"], t, "ohl") for t in range(4)]
-    first = 2 * S // L["we"]
+    order = L["early"] + L["late"]
     wait(act, "su", "ldx")
     for t in range(4):
-        gather(act, "ga", L["self"], CAP, "su", t, "gs")
-    wait(vec, "ldx")
-    for sem, off, part, n, ev, qev in (("a_li", "li", L["early"], L["ne"], "ge", "qearly"),
-                                       ("a_lj", "lj", L["late"], L["nl"], "gl", "qlate")):
+        gather(act, "ga", L["na"] - CAP, CAP, T["su"][:, 0:K], t, "gs")
+    wait(vec, "ldx", "pad", "gs")
+    steps = [("a_li", "li", 0, "ga", L["pad"], L["ne"], "early")]
+    steps += [("a_l%d" % k, "lj", k, "gx", MIN - k * L["xw"], L["xw"], "late%d" % k) for k in range(2)]
+    held = []
+
+    def finish(made, ev, tag, *where):
+        wait(vec, made)
+        quantise(*where, ev)
+        wait(g, ev)
+        send_all(tag)
+
+    for sem, off, k, tile, a, n, tag in steps:
         wait(vec, sem)
         wait(act, sem)
         for t in (0, 1):
-            gather(vec, part[0], part[3], n, off, t, ev)
-            gather(act, part[0], part[3], n, off, t + 2, ev)
-        wait(vec, ev)
-        if part[0] == "ga":
-            wait(vec, "gs")
-            if L["pad"]:
-                wait(vec, "pad")
-        w = L["na"] if part[0] == "ga" else L["nx"]
-        inc(vec.quantize_mx(T[part[1]][:, 0:w], T[part[2]][:, 0:w], T[part[0]][:, 0:4 * w]), qev)
-        wait(g, qev)
-        send_all("early" if ev == "ge" else "late")
-        if ev == "ge":
+            for q in (vec, act):
+                gather(q, tile, a, n, T[off][:, HALF * k // 16:(HALF * k + n) // 16], t + 2 * (q is act), "g" + tag)
+            if held:
+                finish(*held.pop())
+        if tag == "early":
+            held.append(("g" + tag, "q" + tag, tag, "ac", L["at"], "ga", 0, L["na"]))
+        else:
+            held.append(("g" + tag, "q" + tag, tag, L["xbuf"], MIN * (1 - k), "gx", MIN * (1 - k), MIN))
+        if tag != "late0":
+            finish(*held.pop())
+        if tag == "early" and not L["wide"]:
             wait(act, "oo")
-            halve(jobs[:first])
-        else:
-            halve(jobs[first:])
-    wait(vec, "diag")
-    for b in range(4):
-        inc(vec.quantize_mx(T["qe"][:, 128 * b:128 * b + 128], T["qes"][:, 128 * b:128 * b + 128], T["diag"][:, 3 - b:515 - b]), "qe")
+            halve(order[0])
+    wait(act, "oo")
+    for k in order[0 if L["wide"] else 1:]:
+        halve(k)
 
-    def unpack(ps, lo, hi, ev):
+    wait(ten, "qe", "qearly")
+    for n, k in enumerate(order):
+        ps = ("pe", "pl")[n % 2]
+        cols = sorted((L["col"][q], CAP * pos[q]) for q in range(N) if pos[q] // 2 == k)
+        lo = max(cols[0][0] - PAD, 0)
+        runs = [(cols[0], HALF)] if cols[0][1] < cols[1][1] else [(cols[0], CAP), (cols[1], CAP)]
+        if n > 1:
+            wait(ten, "mq%d" % order[n - 2])
+        wait(ten, "a_c%d" % k)
         for b in range(4):
-            inc(ten.matmul_mx(T[ps][:, 512 * b:512 * b + hi - lo], T["qe"][:, 128 * b:128 * b + 128],
-                              T["qes"][:, 128 * b:128 * b + 128], T["ac"][:, lo:hi], T["acs"][:, lo:hi], True, True), ev % b)
-
-    def sums(ps, runs, ev, done):
+            inc(ten.matmul_mx(T[ps][:, 512 * b:512 * b + MIN], T["qe"][:, 128 * b:128 * b + 128], T["qes"][:, 128 * b:128 * b + 128],
+                              T["ac"][:, lo:lo + MIN], T["acs"][:, lo:lo + MIN], True, True), "un%d%d" % (k, b))
+        if k == L["late"][0]:
+            wait(vec, *["mq%d" % m for m in L["early"]])
+        wait(vec, "oh%d" % k)
         for b in range(4):
-            wait(vec, ev % b)
-            for a, f, n in runs:
-                inc(vec.tensor_tensor(T["mt"][:, 4 * f + b:4 * (f + n):4], T[ps][:, 512 * b + a:512 * b + a + n],
-                                      T["oh"][:, F_W * b + f:F_W * b + f + n], add), done)
-        wait(vec, done)
-
-    lo, hi = min(L["self"], L["lin"] - MIN), L["lin"]
-    wait(ten, "qe", "qlate" if L["early_is_x"] else "qearly", "a_ce")
-    unpack("pe", lo, hi, "me%d")
-    runs = []
-    for q, a in sorted([(r, L["self"])] + [(q, L["ein"] + CAP * i) for i, q in enumerate(D)], key=lambda v: pos[v[0]]):
-        if runs and runs[-1][0] + runs[-1][2] == a - lo:
-            runs[-1][2] += CAP
-        else:
-            runs.append([a - lo, CAP * pos[q], CAP])
-    wait(vec, "ohe")
-    sums("pe", runs, "me%d", "mae")
-    we, wl = max(L["we"], MIN), max(L["wl"], MIN)
-    inc(vec.quantize_mx(T["nb"][:, OWN_AT:OWN_AT + we], T["nbs"][:, OWN_AT:OWN_AT + we],
-                        T["mt"][:, 4 * L["e0"]:4 * (L["e0"] + we)]), "mqe")
-    wait(g, "mqe")
-    send_all("me")
-
-    end = L["lin"] + L["nl"]
-    wait(ten, "a_cl")
-    unpack("pl", end - wl, end, "ml%d")
-    wait(vec, "ohl")
-    sums("pl", [[wl - L["wl"], L["l0"], L["wl"]]], "ml%d", "mal")
-    a = L["l0"] + L["wl"] - wl
-    inc(vec.quantize_mx(T["ql"][:, 0:wl], T["qls"][:, 0:wl], T["mt"][:, 4 * a:4 * (a + wl)]), "mql")
-    wait(g, "mql")
-    send_all("ml")
+            wait(vec, "un%d%d" % (k, b))
+            for (a, f), w in runs:
+                inc(vec.tensor_tensor(T["mt"][:, 4 * (PAD + f) + b:4 * (PAD + f + w):4], T[ps][:, 512 * b + a - lo:512 * b + a - lo + w],
+                                      T["oh"][:, F_W * b + f:F_W * b + f + w], add), "ma%d" % k)
+            if held:
+                finish(*held.pop())
+        skip = PAD if k == 0 or [k] == L["late"] else 0
+        buf, a = ("nb", OWN_AT - L["e0"]) if k in L["early"] else ("ql", PAD - L["l0"])
+        held.append(("ma%d" % k, "mq%d" % k, "m%d" % k, buf, a + HALF * k - skip, "mt", PAD + HALF * k - skip, MIN))
+        if k not in L["late"][:-1]:
+            finish(*held.pop())
     wait(vec, "ldwt")
-    inc(vec.quantize_mx(T["wq"][:], T["wqs"][:], T["wt"][:]), "wq")
+    quantise("wq", 0, "wt", 0, 128, "wq")
 
-    def product(ps, bank, buf, a, n, w, ev):
+    def product(ps, bank, buf, a, w, ev):
         inc(ten.matmul_mx(T[ps][:, 512 * bank:512 * bank + w], T["wq"][:], T["wqs"][:], T[buf][:, a:a + w], T[buf + "s"][:, a:a + w],
                           True, True), ev)
 
@@ -440,9 +466,10 @@ def rank_program(g, core, T, topo):
         wait(q, "yg%d" % i)
         inc(q.dma_start(T.y[:, S * i:S * i + S], T["yb"][:, S * i:S * i + S]), "yst", 16)
 
-    wait(ten, "wq", "mqe", "mql")
-    product("pe", 0, "nb", OWN_AT, L["we"], we, "ye1")
-    product("pe", 1, "ql", 0, L["wl"], wl, "yl1")
+    we, wl = max(L["we"], MIN), max(L["wl"], MIN)
+    wait(ten, "wq", *["mq%d" % k for k in order])
+    product("pe", 0, "nb", OWN_AT, we, "ye1")
+    product("pe", 1, "ql", PAD + L["wl"] - wl, wl, "yl1")
     wait(act, "ye1")
     move(act, T["yt1"][:, L["e0"]:L["e0"] + L["we"]], T["pe"][:, 0:L["we"]], "ce1")
     wait(act, "yl1")
@@ -451,9 +478,14 @@ def rank_program(g, core, T, topo):
     pick(act, 1, "so", 0, S)
     store(syn, 1)
 
-    sides = sorted([(0, "l", (r - 1) % N), (2, "r", (r + 1) % N)], key=lambda v: v[2] in X)
-    alike = (sides[0][2] in X) == (sides[1][2] in X)
+    def lateness(q):
+        return 2 if not lay[q]["wide"] else int(q in lay[cross[q][0]]["serve"][1])
+
+    sides = sorted([(0, "l", (r - 1) % N), (2, "r", (r + 1) % N)], key=lambda v: lateness(v[2]))
     for k, (ps, ev, cev) in enumerate((("pe", "ye%d", "ce%d"), ("pl", "yl%d", "cl%d"))):
+        if k == 1:
+            for e in (vec, act):
+                wait(e, "ce0", "ce2", "a_sl", "a_sr")
         for j, (i, n, q) in enumerate(sides):
             Q = lay[q]
             at, f, w = landing(Q, i)[k], Q[("e0", "l0")[k]], Q[("we", "wl")[k]]
@@ -461,17 +493,16 @@ def rank_program(g, core, T, topo):
             skip = wide - w if i == 2 else 0
             bank = 2 * (1 - k) + j
             wait(ten, "a_" + n + "el"[k])
-            product(ps, bank, "nb", at - skip, w, wide, ev % i)
+            product(ps, bank, "nb", at - skip, wide, ev % i)
             eng = vec if k == 0 or j == 1 else act
             wait(eng, ev % i)
             move(eng, T["yt%d" % i][:, f:f + w], T[ps][:, 512 * bank + skip:512 * bank + skip + w], cev % i)
-            if k == 1:
-                shares = [(eng, 0, S)] if alike or j == 0 else [(vec, 0, S // 2), (act, S // 2, S // 2)]
-                for e, a, m in shares:
-                    wait(e, "ce%d" % i, "cl%d" % i, "a_s" + n)
-                    pick(e, i, "s" + n, a, m)
-                store(act if eng is act else syn, i)
-    wait(g, "yst", "sent")
+    for i, n, q in sides:
+        for e, a in ((vec, 0), (act, S // 2)):
+            wait(e, "cl%d" % i)
+            pick(e, i, "s" + n, a, S // 2)
+        store(syn, i)
     for name in count:
-        if name not in waited:
+        if name not in waited and name != "yst":
             wait(g, name)
+    wait(g, "yst")

from concourse.bass import DstId, RemoteDMATransfer
from concourse.mybir import dt, AluOpType, ActivationFunctionType

N, T_COLS, S, CAP = 6, 512, 192, 48
K = CAP // 16
KS = S // 16
W4 = 4 * T_COLS
F_W = N * CAP
MIN = 128
HALF = 2 * CAP
PAD = MIN - HALF
CHUNKS = F_W // HALF
OWN_AT = F_W + PAD
RIGHT_AT = OWN_AT + S + PAD
NB_W = RIGHT_AT + F_W
AC_W = 2 * MIN + S + CAP + 2 * HALF

X4, U8 = "float8_e4m3fn_x4", "uint8"
SCRATCH = {
    "xs": ("sbuf", [128, W4], "bfloat16"),
    "wt": ("sbuf", [128, 512], "bfloat16"),
    "wl": ("sbuf", [128, K * N], "int32"),
    "ls": ("sbuf", [128, 2 * KS], "int32"),
    "wu": ("sbuf", [128, K * N], "uint16"),
    "su": ("sbuf", [128, 4], "uint16"),
    "ou": ("sbuf", [128, KS], "uint16"),
    "so": ("sbuf", [128, KS], "uint16"),
    "sm": ("sbuf", [128, KS], "uint16"),
    "oo": ("sbuf", [128, K * N], "uint16"),
    "t0": ("sbuf", [128, KS], "int32"),
    "t1": ("sbuf", [128, KS], "int32"),
    "t2": ("sbuf", [128, KS], "int32"),
    "t3": ("sbuf", [128, KS], "int32"),
    "t4": ("sbuf", [128, KS], "int32"),
    "t5": ("sbuf", [128, KS], "int32"),
    "t6": ("sbuf", [128, KS], "int32"),
    "cnt": ("sbuf", [128, T_COLS], "float32"),
    "pcol": ("sbuf", [128, 1], "float32"),
    "m0": ("sbuf", [128, 16], "int32"),
    "m1": ("sbuf", [128, 16], "int32"),
    "m16": ("sbuf", [128, 16], "float32"),
    "keep": ("sbuf", [128, F_W], "bfloat16"),
    "orow": ("sbuf", [128, S], "float32"),
    "omask": ("sbuf", [128, S], "float32"),
    "rrow": ("sbuf", [128, F_W], "float32"),
    "rsum": ("sbuf", [128, F_W], "float32"),
    "li": ("sbuf", [128, 12], "uint16"),
    "lj": ("sbuf", [128, 12], "uint16"),
    "sl": ("sbuf", [128, KS], "uint16"),
    "sr": ("sbuf", [128, KS], "uint16"),
    "diag": ("sbuf", [128, 516], "bfloat16"),
    "qe": ("sbuf", [128, 4 * MIN], X4),
    "qes": ("sbuf", [128, 4 * MIN], U8),
    "qx": ("sbuf", [128, 2 * MIN], X4),
    "qxs": ("sbuf", [128, 2 * MIN], U8),
    "wq": ("sbuf", [128, 128], X4),
    "wqs": ("sbuf", [128, 128], U8),
    "ga": ("sbuf", [128, 4 * S], "bfloat16"),
    "gx": ("sbuf", [128, 4 * 2 * MIN], "bfloat16"),
    "ac": ("sbuf", [128, AC_W], X4),
    "acs": ("sbuf", [128, AC_W], U8),
    "oh": ("sbuf", [128, 4 * F_W], "bfloat16"),
    "mt": ("sbuf", [128, 4 * (F_W + 2 * PAD)], "bfloat16"),
    "nb": ("sbuf", [128, NB_W], X4),
    "nbs": ("sbuf", [128, NB_W], U8),
    "ql": ("sbuf", [128, 2 * MIN], X4),
    "qls": ("sbuf", [128, 2 * MIN], U8),
    "yt0": ("sbuf", [128, F_W], "float32"),
    "yt1": ("sbuf", [128, F_W], "float32"),
    "yt2": ("sbuf", [128, F_W], "float32"),
    "yb": ("sbuf", [128, 3 * S], "float32"),
    "rl": ("sbuf", [128, K * N], "uint16"),
    "rs": ("sbuf", [128, KS], "uint16"),
    "rc": ("sbuf", [128, HALF], X4),
    "rcs": ("sbuf", [128, 4 * HALF], U8),
    "rd": ("sbuf", [128, CAP], X4),
    "rds": ("sbuf", [128, 4 * CAP], U8),
    "ra": ("sbuf", [128, S], X4),
    "ras": ("sbuf", [128, S], U8),
    "rm": ("sbuf", [128, HALF], X4),
    "rms": ("sbuf", [128, S], U8),
    "pe": ("psum", [128, 2048], "float32"),
    "pl": ("psum", [128, 2048], "float32"),
}
CODES = {k for k, v in SCRATCH.items() if v[2] == X4}
ARRIVALS = ["a_li", "a_l0", "a_l1", "a_sl", "a_sr", "a_c0", "a_c1", "a_c2", "a_le", "a_re", "a_ll", "a_rl",
            "r_l", "r_s", "r_d", "r_c", "r_a", "r_as", "r_m", "r_ms"]
EVENTS = (["ldw", "ldx", "ldl", "ldwt", "z0", "z1", "z2", "pad", "io0", "io1", "io2", "cnt", "diag", "m1", "m16", "wu", "su",
           "d1", "d2", "ou", "s1", "s2", "s3", "s4", "so", "sm", "orow", "omask", "rrow", "rsum", "oo", "qe", "gs",
           "wq", "yst", "sent"]
          + [s + t for s in "gq" for t in ("early", "late0", "late1")]
          + [s % k for s in ("ma%d", "mq%d", "oh%d") for k in range(CHUNKS)]
          + ["un%d%d" % (k, b) for k in range(CHUNKS) for b in range(4)]
          + [s % i for s in ("ye%d", "yl%d", "ce%d", "cl%d", "yg%d") for i in range(3)])
SEMAPHORES = ARRIVALS + EVENTS


def deal(engines, k):
    n = len(engines) // k
    return [engines[i * n:i * n + n] for i in range(k)]


def orders(items):
    if len(items) < 2:
        return [list(items)]
    return [[v] + rest for i, v in enumerate(items) for rest in orders(items[:i] + items[i + 1:])]


def jumps(pos):
    return [(j, pos[j] - pos[j - 1] - 1) for j in range(1, N) if pos[j] - pos[j - 1] != 1]


def groups(cores, topo):
    near = [q for q in range(N) if q == 0 or topo.may_write(cores[0], cores[q])]
    far = [q for q in range(N) if q not in near]
    wide, narrow = sorted((near, far), key=len, reverse=True)
    order = min((a + b for a in orders(wide) for b in orders(narrow)), key=lambda o: len(jumps([o.index(q) for q in range(N)])))
    direct = [[q for q in order if q != r and topo.may_write(cores[r], cores[q])] for r in range(N)]
    cross = [[q for q in order if q != r and q not in direct[r]] for r in range(N)]
    return direct, cross, [order.index(q) for q in range(N)]


def layout(r, direct, cross, pos):
    ne, nl = CAP * len(direct[r]), CAP * len(cross[r])
    na = max(ne + CAP, MIN)
    pad, wide = na - CAP - ne, ne > nl
    at = 2 * MIN if wide else HALF
    mine = pos[r] // 2
    rest = [k for k in range(CHUNKS) if k != mine]
    base = {rest[0]: at + na + CAP, rest[1]: at + na + CAP + HALF if wide else 0}
    col = [base[pos[q] // 2] + CAP * (pos[q] % 2) if pos[q] // 2 != mine else at + na - CAP * (q == r) for q in range(N)]
    early = [k for k in [mine] + rest if any(pos[q] // 2 == k for q in direct[r])]
    late = [k for k in (rest if pos[r] % 2 == 0 else rest[::-1]) if k not in early]
    h = len(cross[r]) // 2
    serve = [cross[r][:h], cross[r][h:]]
    if wide and pos[serve[0][0]] % 2 != mine:
        serve = serve[::-1]
    if not wide:
        serve.sort(key=lambda some: -sum((q + d) % N in cross[q] for q in some for d in (1, -1)))
    return {"serve": serve, "xbuf": "ac" if wide else "qx", "xw": h * CAP, "na": na, "pad": pad, "at": at, "wide": wide, "col": col,
            "ne": ne, "early": early, "late": late,
            "e0": HALF * min(early), "we": HALF * len(early), "l0": HALF * min(late), "wl": HALF * len(late)}


def landing(L, side):
    return (L["wl"], 0) if side == 0 else (RIGHT_AT, RIGHT_AT + L["we"])


def make_plan(cores, topo):
    direct, cross, pos = groups(cores, topo)
    lay = [layout(r, direct, cross, pos) for r in range(N)]
    calls, due = {}, {}

    def call(core, tag, trs):
        if trs:
            calls.setdefault(core, []).append((tag, trs))
        for to, eng, src, dst, sem in trs:
            due[(to, sem)] = due.get((to, sem), 0) + len(eng)

    for r in range(N):
        c, L = cores[r], lay[r]
        D, X = direct[r], cross[r]
        ports = [p for p in topo.cores_of(c) if p != c and topo.may_write(p, cores[X[0]])]
        near = [p for p in ports if topo.die(p) == topo.die(c)]
        far = [p for p in ports if topo.die(p) != topo.die(c)]
        rel = [near[0], far[0], far[1], near[1]]
        out = topo.engines(c, cores[D[0]])
        every = topo.engines(c, rel[0])
        inside = [e for e in every if e not in out]
        ways = [((r + 1) % N, 0, "l"), ((r - 1) % N, 2, "r")]

        def away(p):
            return topo.engines(p, cores[X[0]])

        h, sh = len(X) // 2, deal(inside, 2)
        asked = sorted(enumerate(X), key=lambda v: r in lay[v[1]]["serve"][1])
        for n in range(h):
            call(c, "list", [(rel[i], sh[m], ("wu", K * q, K * q + K), ("rl", 0, K), "r_l")
                             for m, (i, q) in enumerate(asked[2 * n:2 * n + 2])])
        for i, q in enumerate(X):
            a = [2 * K * n + K * some.index(r) for n, some in enumerate(lay[q]["serve"]) if r in some][0]
            call(rel[i], "r_l", [(cores[q], away(rel[i]), ("rl", 0, K), ("lj", a, a + K), "a_l%d" % (a // (2 * K)))])
        third = [q for q in D if (pos[q] - pos[r]) % (len(D) + 1) == 2]
        pair = sorted((q for q in D if q not in third), key=lambda q: pos[q] // 2 != pos[r] // 2)
        for some in (pair, third):
            sh = deal(out, max(len(some), 1))
            call(c, "list", [(cores[q], sh[i], ("wu", K * q, K * q + K),
                              ("li", K * direct[q].index(r), K * direct[q].index(r) + K), "a_li") for i, q in enumerate(some)])
        sh = deal(inside, 2)
        call(c, "slot", [(rel[3 - i], sh[i], ("so", 0, KS), ("rs", 0, KS), "r_s") for i in range(2)])
        for i, (q, side, n) in enumerate(ways):
            call(rel[3 - i], "r_s", [(cores[q], away(rel[3 - i]), ("rs", 0, KS), ("s" + n, 0, KS), "a_s" + n)])

        def place(buf, q):
            return (buf, lay[q]["col"][r], lay[q]["col"][r] + CAP), "a_c%d" % (pos[r] // 2)

        def source(buf, q):
            a = L["at"] + L["pad"] + CAP * D.index(q)
            return (buf, a, a + CAP)

        for b, (buf, stop) in enumerate((("ac", "rd"), ("acs", "rds"))):
            some = [(v, rel[2 * n + (b + n) % 2]) for n, v in enumerate(pair[1:] + third)]
            call(c, "early", [(p, deal(inside, 2)[n], source(buf, v), (stop, 0, CAP), "r_d") for n, (v, p) in enumerate(some)]
                 + [(cores[pair[0]], out, source(buf, pair[0])) + place(buf, pair[0])])
            for v, p in some:
                call(p, "r_d", [(cores[v], away(p), (stop, 0, CAP)) + place(buf, v)])
        j, w = pos[r], L["xw"]
        for n, some in enumerate(L["serve"]):
            a = MIN - n * w
            if L["wide"]:
                ps = [rel[2 * b + (j + n) % 2] for b in (0, 1)]
                call(c, "late%d" % n, [(ps[0], inside, ("ac", a, a + w), ("rc", 0, w), "r_c"),
                                       (ps[1], out, ("acs", a, a + 4 * w), ("rcs", 0, 4 * w), "r_c")])
                for p, stop, land in zip(ps, ("rc", "rcs"), ("ac", "acs")):
                    call(p, "r_c", [(cores[some[0]], away(p), (stop, 0, CAP)) + place(land, some[0])])
            elif n == 0:
                for b, s in enumerate(("", "s")):
                    ps = [rel[2 * b + (j + m) % 2] for m in range(h)]
                    call(c, "late0", [(p, deal(every, h)[m], ("qx" + s, a + CAP * m, a + CAP * m + CAP), ("rc" + s, 0, CAP), "r_c")
                                      for m, p in enumerate(ps)])
                    for p, q in zip(ps, some):
                        call(p, "r_c", [(cores[q], away(p), ("rc" + s, 0, CAP)) + place("ac" + s, q)])
            else:
                for m, q in enumerate(some):
                    ps, at = [rel[2 * b + (j + m) % 2] for b in (0, 1)], a + CAP * m
                    lo = min(at, 2 * MIN - 4 * CAP)
                    call(c, "late1", [(ps[0], inside, ("qx", at, at + CAP), ("rd", 0, CAP), "r_d"),
                                      (ps[1], out, ("qxs", lo, lo + 4 * CAP), ("rds", 0, 4 * CAP), "r_d")])
                    call(ps[0], "r_d", [(cores[q], away(ps[0]), ("rd", 0, CAP)) + place("ac", q)])
                    call(ps[1], "r_d", [(cores[q], away(ps[1]), ("rds", at - lo, at - lo + CAP)) + place("acs", q)])

        last, n = "m%d" % L["early"][-1], len(L["late"])
        pieces = [(last, "nb", OWN_AT, L["we"], 0, 0, 0, "ra"), (last, "nbs", OWN_AT, L["we"], 0, 0, 1, "ras")]
        pieces += [("m%d" % m, "ql", PAD, HALF, 1, HALF * m - L["l0"], i, "rm") for i, m in enumerate(L["late"])]
        pieces += [("m%d" % L["late"][-1], "qls", PAD, L["wl"], 1, 0, n % 2, "rms")]
        for tag, src, a, w, k, off, by, stop in pieces:
            straight = k == 1 and all(q in D for q, side, name in ways)
            sh, sem, trs = deal(out if straight else every, 2), "r_" + stop[1:], []
            for i, (q, side, name) in enumerate(ways):
                p, at = rel[i + 2 * by], landing(L, side)[k] + off
                end = (("nb" if src in CODES else "nbs", at, at + w), "a_" + name + "el"[k])
                if straight:
                    trs.append((cores[q], sh[i], (src, a + off, a + off + w)) + end)
                else:
                    trs.append((p, sh[i], (src, a + off, a + off + w), (stop, 0, w), sem))
                    call(p, sem, [(cores[q], away(p), (stop, 0, w)) + end])
            call(c, tag, trs)
    return direct, cross, pos, lay, calls, due


def rank_program(g, core, T, topo):
    direct, cross, pos, lay, calls, due = make_plan(T.cores, topo)
    mine = calls.get(core)
    if mine is None:
        return
    count, waited = {}, set()

    def view(v):
        a = T[v[0]][:, v[1]:v[2]]
        return a.bitcast(dt.uint8) if v[0] in CODES else a

    def inc(ins, name, n=1):
        ins.then_inc(T.sem[name], n)
        count[name] = count.get(name, 0) + n

    def wait(q, *names):
        for name in names:
            q.wait_ge(T.sem[name], due[(core, name)] if (core, name) in due else count[name])
            waited.add(name)

    def send(trs):
        out = []
        for to, eng, src, dst, sem in trs:
            rid, pid = topo.addr(to, core)
            out.append(RemoteDMATransfer(dst_ids=[DstId(rid=rid, pnc=pid)], dma_engine_mask=sum(1 << e for e in eng),
                                         remote_sem=T.sem[sem], src=view(src), dst=view(dst)))
            count["sent"] = count.get("sent", 0) + len(eng)
        g.remote_dma_fused(out, local_sem=T.sem["sent"])

    def send_all(tag):
        for t, trs in mine:
            if t == tag:
                send(trs)

    r = T.rank_of(core)
    if r is None:
        for tag, trs in mine:
            wait(g, tag)
            send(trs)
        wait(g, "sent")
        return

    vec, act, ten, syn = g.vector, g.scalar, g.tensor, g.sync
    L, D, X = lay[r], direct[r], cross[r]
    copy, ident = ActivationFunctionType.Copy, ActivationFunctionType.Identity
    add, mult = AluOpType.add, AluOpType.mult

    def move(q, dst, src, ev):
        inc(q.tensor_copy(dst, src) if q is vec else q.activation(dst, src, copy), ev)

    def quantise(buf, a, tile, b, w, ev):
        inc(vec.quantize_mx(T[buf][:, a:a + w], T[buf + "s"][:, a:a + w], T[tile][:, 4 * b:4 * (b + w)]), ev)

    for k in range(4):
        inc((syn if k < 2 else act).dma_start(T["wl"][16 * k:16 * k + 16, :], T.want[:]), "ldw", 16)
    for k in range(2):
        inc(act.dma_start(T["ls"][16 * k:16 * k + 16, 0:KS], T.own[:]), "ldl", 16)
        inc(syn.dma_start(T["ls"][16 * k:16 * k + 16, KS:2 * KS], T.slot[:]), "ldl", 16)
    inc(syn.dma_start(T["xs"][:], T.x[:]), "ldx", 16)
    wait(syn, "a_li")
    inc(syn.dma_start(T["wt"][:], T.w[:]), "ldwt", 16)

    inc(g.iota(T["m0"][:], [[1, 16]], 128, -1), "io2")
    inc(g.iota(T["cnt"][:, 0:128], [[1, 128]], 0, 0, allow_small_or_imprecise_dtypes=True), "io0")
    inc(g.iota(T["pcol"][:], [[1, 1]], 0, 1, allow_small_or_imprecise_dtypes=True), "io1")
    inc(vec.memset(T["diag"][:], 0.0), "z0")
    inc(vec.memset(T["keep"][:], 1.0), "z1")
    wait(vec, "z1", "io2")
    inc(vec.memset(T["keep"][:, 0:F_W:16], 0.0), "z2")
    inc(vec.tensor_scalar(T["m1"][:], T["m0"][:], 15, None, AluOpType.bitwise_and), "m1")
    wait(vec, "m1")
    inc(vec.tensor_scalar(T["m16"][:], T["m1"][:], 0.0, None, AluOpType.is_equal), "m16")
    wait(act, "io0")
    for k in range(1, T_COLS // 128):
        inc(act.activation(T["cnt"][:, 128 * k:128 * k + 128], T["cnt"][:, 0:128], ident, bias=float(128 * k)), "cnt")
    wait(act, "cnt")
    inc(act.activation(T["rrow"][:], T["cnt"][:, 0:F_W], copy, scale=0.0), "z2")

    wait(vec, "ldw")
    for h in (0, 64):
        inc(vec.tensor_scalar(T["wu"][h:h + 64, :], T["wl"][0:64, :], 0.0, 4.0, AluOpType.max, mult), "wu")
    wait(g, "wu")
    send_all("list")
    wait(vec, "z0", "io0", "io1")
    inc(vec.tensor_scalar(T["diag"][:, 3:515:4], T["cnt"][:, 0:128], T["pcol"][:], 0.5, AluOpType.is_equal, mult), "diag")

    def constant(b):
        inc(vec.quantize_mx(T["qe"][:, 128 * b:128 * b + 128], T["qes"][:, 128 * b:128 * b + 128], T["diag"][:, 3 - b:515 - b]), "qe")

    wait(vec, "ldl")
    inc(vec.tensor_copy(T["ls"][32:64, :], T["ls"][0:32, :]), "d1")
    wait(vec, "wu")
    inc(vec.tensor_copy(T["su"][:, 0:K], T["wu"][:, K * r:K * r + K]), "su")
    wait(vec, "d1")
    inc(vec.tensor_copy(T["ls"][64:128, :], T["ls"][0:64, :]), "d2")
    wait(vec, "diag")
    constant(0)
    wait(vec, "d2")
    own, slot = T["ls"][:, 0:KS], T["ls"][:, KS:2 * KS]
    inc(vec.tensor_copy(T["ou"][:], own), "ou")
    inc(vec.tensor_scalar(T["t0"][:], slot, 15, None, AluOpType.bitwise_and), "s1")
    terms = []
    for (j, d), tmp in zip(jumps(pos), ("t1", "t2", "t3")):
        inc(vec.tensor_scalar(T[tmp][:], slot, float(CAP * j), float(CAP * d), AluOpType.is_ge, mult), "s1")
        terms.append(tmp)
    wait(vec, "s1")
    inc(vec.tensor_copy(T["sm"][:], T["t0"][:]), "sm")
    acc = slot
    for tmp, to, ev in zip(terms, ("t4", "t5", "t6"), ("s2", "s3", "s4")):
        inc(vec.tensor_tensor(T[to][:], acc, T[tmp][:], add), ev)
        wait(vec, ev)
        acc = T[to][:]
    inc(vec.tensor_scalar(T["so"][:], acc, float(CAP * pos[0]), None, add), "so")
    wait(g, "so")
    send_all("slot")
    wait(act, "cnt", "ou")
    move(act, T["orow"][:], T["cnt"][:, 0:T_COLS].indirect(T["ou"][:, 0:KS]), "orow")
    pads = [("mt", 0, PAD), ("mt", PAD + L["e0"] + L["we"], PAD), ("gx", 0, MIN - L["xw"]), ("gx", MIN + L["xw"], MIN - L["xw"])]
    for buf, a, w in pads + ([("ga", 0, L["pad"])] if L["pad"] else []):
        inc(act.activation(T[buf][:, 4 * a:4 * (a + w)], T["cnt"][:, 0:4 * w], copy, scale=0.0), "pad")
    wait(vec, "orow", "sm", "m16")
    inc(vec.tensor_tensor(T["omask"][:], T["m16"][:, 0:16].indirect(T["sm"][:, 0:KS]), T["orow"][:], mult), "omask")
    constant(1)
    wait(vec, "omask", "so", "z2")
    move(vec, T["rrow"][:, 0:F_W].indirect(T["so"][:, 0:KS]), T["omask"][:], "rrow")
    constant(2)
    wait(vec, "rrow")
    inc(vec.tensor_tensor_scan(T["rsum"][:], T["keep"][:], T["rrow"][:], 0.0, mult, add), "rsum")
    constant(3)
    wait(vec, "rsum")
    inc(vec.tensor_scalar(T["oo"][:], T["rsum"][:, 15:F_W:16], 4.0, None, mult), "oo")

    def gather(q, tile, a, n, off, t, name):
        move(q, T[tile][:, 4 * a + t:4 * (a + n):4], T["xs"][:, t:W4].indirect(off), name)

    def halve(k):
        a = HALF * k
        for t in range(4):
            inc(act.activation(T["oh"][:, F_W * t + a:F_W * t + a + HALF],
                               T["xs"][:, t:W4].indirect(T["oo"][:, a // 16:(a + HALF) // 16]), copy, scale=0.5), "oh%d" % k)

    order = L["early"] + L["late"]
    wait(act, "su", "ldx")
    for t in range(4):
        gather(act, "ga", L["na"] - CAP, CAP, T["su"][:, 0:K], t, "gs")
    wait(vec, "ldx", "pad", "gs")
    steps = [("a_li", "li", 0, "ga", L["pad"], L["ne"], "early")]
    steps += [("a_l%d" % k, "lj", k, "gx", MIN - k * L["xw"], L["xw"], "late%d" % k) for k in range(2)]
    held = []

    def finish(made, ev, tag, *where):
        wait(vec, made)
        quantise(*where, ev)
        wait(g, ev)
        send_all(tag)

    for sem, off, k, tile, a, n, tag in steps:
        wait(vec, sem)
        wait(act, sem)
        for t in (0, 1):
            for q in (vec, act):
                gather(q, tile, a, n, T[off][:, HALF * k // 16:(HALF * k + n) // 16], t + 2 * (q is act), "g" + tag)
            if held:
                finish(*held.pop())
        if tag == "early":
            held.append(("g" + tag, "q" + tag, tag, "ac", L["at"], "ga", 0, L["na"]))
        else:
            held.append(("g" + tag, "q" + tag, tag, L["xbuf"], MIN * (1 - k), "gx", MIN * (1 - k), MIN))
        if tag != "late0":
            finish(*held.pop())
        if tag == "early" and not L["wide"]:
            wait(act, "oo")
            halve(order[0])
    wait(act, "oo")
    for k in order[0 if L["wide"] else 1:]:
        halve(k)

    wait(ten, "qe", "qearly")
    for n, k in enumerate(order):
        ps = ("pe", "pl")[n % 2]
        cols = sorted((L["col"][q], CAP * pos[q]) for q in range(N) if pos[q] // 2 == k)
        lo = max(cols[0][0] - PAD, 0)
        runs = [(cols[0], HALF)] if cols[0][1] < cols[1][1] else [(cols[0], CAP), (cols[1], CAP)]
        if n > 1:
            wait(ten, "mq%d" % order[n - 2])
        wait(ten, "a_c%d" % k)
        for b in range(4):
            inc(ten.matmul_mx(T[ps][:, 512 * b:512 * b + MIN], T["qe"][:, 128 * b:128 * b + 128], T["qes"][:, 128 * b:128 * b + 128],
                              T["ac"][:, lo:lo + MIN], T["acs"][:, lo:lo + MIN], True, True), "un%d%d" % (k, b))
        if k == L["late"][0]:
            wait(vec, *["mq%d" % m for m in L["early"]])
        wait(vec, "oh%d" % k)
        for b in range(4):
            wait(vec, "un%d%d" % (k, b))
            for (a, f), w in runs:
                inc(vec.tensor_tensor(T["mt"][:, 4 * (PAD + f) + b:4 * (PAD + f + w):4], T[ps][:, 512 * b + a - lo:512 * b + a - lo + w],
                                      T["oh"][:, F_W * b + f:F_W * b + f + w], add), "ma%d" % k)
            if held:
                finish(*held.pop())
        skip = PAD if k == 0 or [k] == L["late"] else 0
        buf, a = ("nb", OWN_AT - L["e0"]) if k in L["early"] else ("ql", PAD - L["l0"])
        held.append(("ma%d" % k, "mq%d" % k, "m%d" % k, buf, a + HALF * k - skip, "mt", PAD + HALF * k - skip, MIN))
        if k not in L["late"][:-1]:
            finish(*held.pop())
    wait(vec, "ldwt")
    quantise("wq", 0, "wt", 0, 128, "wq")

    def product(ps, bank, buf, a, w, ev):
        inc(ten.matmul_mx(T[ps][:, 512 * bank:512 * bank + w], T["wq"][:], T["wqs"][:], T[buf][:, a:a + w], T[buf + "s"][:, a:a + w],
                          True, True), ev)

    def pick(q, i, off, a, n):
        move(q, T["yb"][:, S * i + a:S * i + a + n], T["yt%d" % i][:, 0:F_W].indirect(T[off][:, a // 16:(a + n) // 16]), "yg%d" % i)

    def store(q, i):
        wait(q, "yg%d" % i)
        inc(q.dma_start(T.y[:, S * i:S * i + S], T["yb"][:, S * i:S * i + S]), "yst", 16)

    we, wl = max(L["we"], MIN), max(L["wl"], MIN)
    wait(ten, "wq", *["mq%d" % k for k in order])
    product("pe", 0, "nb", OWN_AT, we, "ye1")
    product("pe", 1, "ql", PAD + L["wl"] - wl, wl, "yl1")
    wait(act, "ye1")
    move(act, T["yt1"][:, L["e0"]:L["e0"] + L["we"]], T["pe"][:, 0:L["we"]], "ce1")
    wait(act, "yl1")
    move(act, T["yt1"][:, L["l0"]:L["l0"] + L["wl"]], T["pe"][:, 512 + wl - L["wl"]:512 + wl], "cl1")
    wait(act, "ce1", "cl1")
    pick(act, 1, "so", 0, S)
    store(syn, 1)

    def lateness(q):
        return 2 if not lay[q]["wide"] else int(q in lay[cross[q][0]]["serve"][1])

    sides = sorted([(0, "l", (r - 1) % N), (2, "r", (r + 1) % N)], key=lambda v: lateness(v[2]))
    for k, (ps, ev, cev) in enumerate((("pe", "ye%d", "ce%d"), ("pl", "yl%d", "cl%d"))):
        if k == 1:
            for e in (vec, act):
                wait(e, "ce0", "ce2", "a_sl", "a_sr")
        for j, (i, n, q) in enumerate(sides):
            Q = lay[q]
            at, f, w = landing(Q, i)[k], Q[("e0", "l0")[k]], Q[("we", "wl")[k]]
            wide = max(w, MIN)
            skip = wide - w if i == 2 else 0
            bank = 2 * (1 - k) + j
            wait(ten, "a_" + n + "el"[k])
            product(ps, bank, "nb", at - skip, wide, ev % i)
            eng = vec if k == 0 or j == 1 else act
            wait(eng, ev % i)
            move(eng, T["yt%d" % i][:, f:f + w], T[ps][:, 512 * bank + skip:512 * bank + skip + w], cev % i)
    for i, n, q in sides:
        for e, a in ((vec, 0), (act, S // 2)):
            wait(e, "cl%d" % i)
            pick(e, i, "s" + n, a, S // 2)
        store(syn, i)
    for name in count:
        if name not in waited and name != "yst":
            wait(g, name)
    wait(g, "yst")
